import numpy as np
import ml_dtypes


def mxq(x, axis, fmt="e4m3"):
    dtype, down = {"e4m3": (ml_dtypes.float8_e4m3fn, 7), "e5m2": (ml_dtypes.float8_e5m2, 14)}[fmt]
    v = np.moveaxis(np.asarray(x, np.float32).astype(ml_dtypes.bfloat16).astype(np.float64), axis, -1)
    blocks = v.reshape(v.shape[:-1] + (-1, 32))
    amax = np.abs(blocks).max(-1, keepdims=True)
    byte = np.maximum(np.where(amax > 0, np.frexp(amax)[1] - 1 + 127, 0) - down, 1)
    scale = np.exp2(byte - 127.0)
    codes = (blocks / scale).astype(np.float32).astype(dtype).astype(np.float64)
    return np.moveaxis((codes * scale).reshape(v.shape), -1, axis)


WIDE = False


def mx_kscale(k):
    if not WIDE:
        return np.ones(k)
    levels = np.array([10, -10, 5, -5, 0])
    if k % 512:
        return np.exp2(np.random.permutation(np.resize(levels, k // 32))).repeat(32)
    a = np.empty((k // 512, 16))
    for p in range(k // 512):
        a[p, :8] = np.random.permutation(np.resize(levels, 8))
        for g in range(8):
            far = levels[np.abs(levels - a[p, g]) >= 10]
            a[p, g + 8] = far[np.random.randint(len(far))]
    return np.exp2(a.ravel()).repeat(32)


def f64(x):
    return np.asarray(x).astype(np.float64)


def striped(idx):
    return np.tile(idx.reshape(-1, 16).T, (8, 1)).astype(np.uint16)


def unstriped(offs):
    return offs[:16].T.reshape(-1).astype(np.int64)


E2M1 = np.array([0.0, 0.5, 1.0, 1.5, 2.0, 3.0, 4.0, 6.0, -0.0, -0.5, -1.0, -1.5, -2.0, -3.0, -4.0, -6.0])


def pack_weight(w, fmt):
    k, n = w.shape
    w = f64(np.asarray(w, np.float32).astype(ml_dtypes.bfloat16)).reshape(k // 32, 32, n)
    amax = np.abs(w).max(1)
    if fmt == "e4m3":
        byte = np.frexp(amax)[1] - 1 + 127 - 7
    else:
        mant, ex = np.frexp(amax / 6.0)
        byte = np.where(mant > 0.5, ex, ex - 1) + 127
    byte = np.clip(np.where(amax > 0, byte, 1), 1, 254)
    scaled = (w * np.exp2(127.0 - byte)[:, None, :]).reshape(k, n).astype(np.float32)
    by_word = np.ascontiguousarray(scaled.reshape(k // 512, 128, 4, n).transpose(0, 1, 3, 2))
    if fmt == "e4m3":
        words = by_word.astype(ml_dtypes.float8_e4m3fn).view(np.uint8)
    else:
        c = by_word.astype(ml_dtypes.float4_e2m1fn).view(np.uint8) & 0xF
        words = (c[..., 0::2] | (c[..., 1::2] << 4)).reshape(k // 512, 128, 2 * n)
    return np.ascontiguousarray(words), np.ascontiguousarray(byte.astype(np.uint8).reshape(k // 512, 16, n))


def unpack_weight(words, scales, fmt):
    g, _, n = scales.shape
    words = np.ascontiguousarray(words).reshape(g, 128, n, -1)
    if fmt == "e4m3":
        vals = words.view(ml_dtypes.float8_e4m3fn).astype(np.float64)
    else:
        nib = np.empty((g, 128, n, 4), np.uint8)
        nib[..., 0::2] = words & 0xF
        nib[..., 1::2] = words >> 4
        vals = E2M1[nib]
    vals = vals * np.repeat(np.exp2(scales.astype(np.float64) - 127.0), 8, axis=1)[..., None]
    return vals.transpose(0, 1, 3, 2).reshape(g * 512, n)


def silu(v):
    return v / (1.0 + np.exp(-np.maximum(v, -700.0)))


K, T, E, C, H, TOP, COPIES = 1024, 768, 4, 256, 512, 2, 192
PAD = 64


def by_expert(wq, xq):
    return np.concatenate([wq[e].T @ xq[:, e * C:(e + 1) * C] for e in range(E)], axis=1)


def setup_inputs():
    n = np.random.standard_normal
    s = mx_kscale(K)
    u = mx_kscale(H)
    left = TOP * T - E * C - COPIES
    deal = np.repeat(np.arange(E + 2), [C] * E + [COPIES, left]).reshape(TOP, T)[:, np.random.permutation(T)]
    deal = np.take_along_axis(deal, np.argsort(np.random.rand(TOP, T), axis=0), axis=0)
    for _ in range(8):
        s_, t_ = np.random.permutation(T).reshape(2, -1); r = np.random.randint(TOP, size=T // 2); x, y = deal[r, s_].copy(), deal[r, t_].copy()
        ok = ~((deal[:, s_] == y).any(0) | (deal[:, t_] == x).any(0)); deal[r[ok], s_[ok]] = y[ok]; deal[r[ok], t_[ok]] = x[ok]
    order = np.lexsort((np.random.rand(TOP * T), deal.reshape(-1)))[:E * C]
    slot_token = order % T
    pos = np.where(deal == E, E * C + np.arange(T), E * C + T + np.arange(T) % PAD).reshape(-1); pos[order] = np.arange(E * C); pos = pos.reshape(TOP, T)
    g = np.random.uniform(0.5, 1.5, (TOP, T)); g = g / g.sum(0)
    xf = n((K, T))
    x = pack_weight(xf * s[:, None], "e4m3")
    w1 = [pack_weight(m, "e2m1") for m in n((E, K, H)) / np.sqrt(K) / s[None, :, None] * u]
    w2 = [pack_weight(m, "e2m1") for m in n((E, H, K)) / np.sqrt(H) / u[None, :, None]]
    return {
        "x_words": x[0],
        "x_scales": x[1],
        "xr": (xf).astype(np.float32),
        "w1_words": np.stack([m[0] for m in w1]),
        "w1_scales": np.stack([m[1] for m in w1]),
        "w2_words": np.stack([m[0] for m in w2]),
        "w2_scales": np.stack([m[1] for m in w2]),
        "gate": np.stack([np.tile(r, (128, 1)) for r in g]).astype(np.float32),
        "offs": striped(slot_token),
        "pos1": striped(pos[0]),
        "pos2": striped(pos[1]),
    }


def reference(x_words, x_scales, xr, w1_words, w1_scales, w2_words, w2_scales, gate, offs, pos1, pos2):
    w1 = np.stack([unpack_weight(w1_words[e], w1_scales[e], "e2m1") for e in range(E)])
    w2 = np.stack([unpack_weight(w2_words[e], w2_scales[e], "e2m1") for e in range(E)])
    idx = unstriped(offs)
    xq = unpack_weight(x_words, x_scales, "e4m3")[:, idx]
    h = silu(by_expert(w1, xq))
    y = by_expert(w2, mxq(h, 0, "e4m3"))
    y = np.concatenate([y, f64(xr), np.zeros((K, PAD))], axis=1)
    out = sum(f64(gate[r, :1]) * y[:, unstriped(p)] for r, p in enumerate((pos1, pos2)))
    return out

@@ -1,0 +1,257 @@
+from contextlib import ExitStack
+
+import concourse.mybir as mybir
+from concourse.masks import make_identity
+
+K, T, E, C, H, PAD = 1024, 768, 4, 256, 512, 64
+S = E * C
+W = S + T + PAD
+P = 128
+NB = K // P
+FLOPS = 2 * 2 * S * K * H
+
+F32 = mybir.dt.float32
+BF16 = mybir.dt.bfloat16
+I32 = mybir.dt.int32
+U32 = mybir.dt.uint32
+U16 = mybir.dt.uint16
+U8 = mybir.dt.uint8
+FP8X4 = mybir.dt.float8_e4m3fn_x4
+FP4X4 = mybir.dt.float4_e2m1fn_x4
+MULT = mybir.AluOpType.mult
+ADD = mybir.AluOpType.add
+SILU = mybir.ActivationFunctionType.Silu
+
+PACK = False
+PE_ADD = 7
+CHUNKS = [(0, 256), (256, 256), (512, 256), (768, 128), (896, 128)]
+VCOPY = ()
+
+
+def tile_moe_cpy_mlp_silu_kernel(
+    tc, x_words, x_scales, xr, w1_words, w1_scales, w2_words, w2_scales, gate, offs, pos1, pos2, out
+):
+    nc = tc.nc
+    with ExitStack() as ctx:
+        lists = ctx.enter_context(tc.tile_pool(name="lists", bufs=1))
+        keep = ctx.enter_context(tc.tile_pool(name="keep", bufs=1))
+        ring = ctx.enter_context(tc.tile_pool(name="ring", bufs=2))
+        deep = ctx.enter_context(tc.tile_pool(name="deep", bufs=4))
+        psum = ctx.enter_context(tc.psum_pool(name="psum", bufs=2))
+        psum_y = ctx.enter_context(tc.psum_pool(name="psum_y", bufs=4))
+
+        offs_t = lists.tile([P, S // 16], U16, name="offs_t")
+        pos_t = [lists.tile([P, T // 16], U16, name=f"pos_t{r}") for r in range(2)]
+
+        xw = [keep.tile([P, T], I32, name=f"xw{s}", align_bytes=64) for s in range(2)]
+        xs = keep.tile([P, T if PACK else 2 * T], U8, name="xs", align_bytes=64)
+        w1 = [keep.tile([P, 2 * 2 * H], U8, name=f"w1_{e}", align_bytes=64) for e in range(E)]
+        w1s = keep.tile([P, E * 2 * H], U8, name="w1s", align_bytes=64)
+        w2 = [keep.tile([P, E * K], U8, name=f"w2_{h}", align_bytes=64) for h in range(2)]
+        w2s = keep.tile([P, E * K], U8, name="w2s", align_bytes=64)
+        g = [keep.tile([P, T], F32, name=f"g{r}") for r in range(2)]
+        y = [keep.tile([P, W], F32, name=f"y{n}") for n in range(NB)]
+        ident = keep.tile([P, P], F32, name="ident")
+        warm = keep.tile([P, 8], F32, name="warm")
+
+        nc.gpsimd.memset(xs[:].bitcast(I32), 0)
+        nc.vector.memset(w1s[:].bitcast(I32), 0)
+        nc.vector.memset(w2s[:].bitcast(I32), 0)
+        make_identity(nc, ident[:])
+        for n in range(NB):
+            nc.gpsimd.memset(y[n][:, S + T : W], 0.0)
+
+        SQ = nc.scalar
+        nc.sync.dma_start(offs_t[:], offs)
+        xs_d = x_scales.bitcast(I32)
+        for q in range(4):
+            if PACK:
+                SQ.dma_start(xs[32 * q : 32 * q + 8, :].bitcast(I32), xs_d[:, 4 * q : 4 * q + 4, :])
+            else:
+                SQ.dma_start(
+                    xs[32 * q : 32 * q + 4, :].bitcast(I32).rearrange("r (s t) -> r s t", s=2),
+                    xs_d[:, 4 * q : 4 * q + 4, :].rearrange("s r t -> r s t"),
+                )
+        for s in range(2):
+            nc.sync.dma_start(xw[s][:], x_words[s].rearrange("p t d -> p (t d)").bitcast(I32))
+        w1s_d = w1_scales.bitcast(I32).rearrange("e s b i -> b (e s) i")
+        for q in range(4):
+            SQ.dma_start(
+                w1s[32 * q : 32 * q + 4, :].bitcast(I32).rearrange("r (a i) -> r a i", a=2 * E),
+                w1s_d[4 * q : 4 * q + 4],
+            )
+        for e in range(E):
+            nc.sync.dma_start(
+                w1[e][:].bitcast(I32).rearrange("p (s i) -> p s i", s=2),
+                w1_words[e].bitcast(I32).rearrange("s p i -> p s i"),
+            )
+        nc.scalar.activation(warm[:], ident[:, 0:8], SILU)
+        w2s_d = w2_scales.bitcast(I32).rearrange("e s b n -> b (e s) n")
+        for q in range(4):
+            SQ.dma_start(
+                w2s[32 * q : 32 * q + 4, :].bitcast(I32).rearrange("r (e n) -> r e n", e=E),
+                w2s_d[4 * q : 4 * q + 4],
+            )
+        w2_d = w2_words.bitcast(I32).rearrange("e s p n -> p (e s) n")
+
+        def load_w2(h):
+            nc.sync.dma_start(
+                w2[h][:].bitcast(I32).rearrange("p (e n) -> p e n", e=E),
+                w2_d[:, :, h * (K // 4) : (h + 1) * (K // 4)],
+            )
+
+        def load_xr(n):
+            nc.sync.dma_start(y[n][:, S : S + T], xr[n * P : (n + 1) * P, :])
+
+        load_w2(0)
+        nc.sync.dma_start(pos_t[0][:], pos1)
+        nc.sync.dma_start(pos_t[1][:], pos2)
+        nc.sync.dma_start(g[0][:], gate[0])
+        load_xr(0)
+        nc.sync.dma_start(g[1][:], gate[1])
+        load_xr(1)
+        load_w2(1)
+        for n in range(2, NB):
+            load_xr(n)
+
+        if PACK:
+            halves = []
+            for a in range(2):
+                both = keep.tile([P, S // 2], U8, name=f"both{a}", align_bytes=64)
+                moved = keep.tile([P, S // 2], U8, name=f"moved{a}", align_bytes=64)
+                nc.vector.memset(moved[:].bitcast(I32), 0)
+                halves.append((both, moved))
+            for a in range(2):
+                both, moved = halves[a]
+                nc.vector.tensor_copy(both[:], xs[:].indirect(offs_t[:, a * 32 : (a + 1) * 32]))
+                for q in range(4):
+                    nc.scalar.dma_start(
+                        moved[32 * q : 32 * q + 4, :].bitcast(I32), both[32 * q + 4 : 32 * q + 8, :].bitcast(I32)
+                    )
+
+        codes = [keep.tile([P, C], U32, name=f"codes{e}", align_bytes=64) for e in range(E)]
+        cs = [keep.tile([P, C], U8, name=f"cs{e}", align_bytes=64) for e in range(E)]
+
+        def second_layer(acc, e, n, lo, size):
+            h, m = divmod(n, NB // 2)
+            nc.tensor.matmul_mx(
+                out=acc,
+                lhsT=w2[h][:, e * K + m * 2 * P : e * K + (m + 1) * 2 * P].bitcast(FP4X4),
+                lhsT_scale=w2s[:, e * K + n * P : e * K + (n + 1) * P],
+                rhs=codes[e][:, lo : lo + size].bitcast(FP8X4),
+                rhs_scale=cs[e][:, lo : lo + size],
+                start=True,
+                stop=True,
+            )
+
+        gathered = {}
+
+        def gather(i):
+            lo, size = CHUNKS[i]
+            idx = offs_t[:, lo // 16 : (lo + size) // 16]
+            xg, sg = [], []
+            for s in range(2):
+                w = keep.tile([P, size], U32, name=f"xg{i}_{s}", align_bytes=64)
+                nc.vector.tensor_copy(w[:], xw[s][:].bitcast(U32).indirect(idx))
+                xg.append(w[:])
+                if PACK:
+                    a, at = divmod(lo, S // 2)
+                    sg.append(halves[a][s][:, at : at + size])
+                else:
+                    b = keep.tile([P, size], U8, name=f"sg{i}_{s}", align_bytes=64)
+                    nc.vector.tensor_copy(b[:], xs[:, s * T : (s + 1) * T].indirect(idx))
+                    sg.append(b[:])
+            gathered[i] = (xg, sg)
+
+        def hidden(i):
+            lo, size = CHUNKS[i]
+            e, at = divmod(lo, C)
+            xg, sg = gathered[i]
+            blocks = size // P
+            hT = psum.tile([P, blocks, 2, P], F32, name="hT", tag="b")
+            for b in range(blocks):
+                pre = psum.tile([P, H], F32, name="pre", tag="a")
+                for s in range(2):
+                    nc.tensor.matmul_mx(
+                        out=pre[:],
+                        lhsT=xg[s][:, b * P : (b + 1) * P].bitcast(FP8X4),
+                        lhsT_scale=sg[s][:, b * P : (b + 1) * P],
+                        rhs=w1[e][:, s * 2 * H : (s + 1) * 2 * H].bitcast(FP4X4),
+                        rhs_scale=w1s[:, (2 * e + s) * H : (2 * e + s + 1) * H],
+                        start=(s == 0),
+                        stop=(s == 1),
+                    )
+                hb = ring.tile([P, H], BF16, name="hb")
+                nc.scalar.activation(
+                    hb[:].rearrange("s (u p d) -> s u p d", u=2, d=2),
+                    pre[:].rearrange("s (p u d) -> s u p d", u=2, d=2),
+                    SILU,
+                )
+                words = hb[:].bitcast(F32)
+                for u in range(2):
+                    nc.tensor.transpose(hT[:, b, u, :], words[:, u * P : (u + 1) * P], ident[:])
+            hq = ring.tile([P, 4 * size], BF16, name="hq", align_bytes=64)
+            dst = hq[:].bitcast(F32).rearrange("p (b s u) -> p b s u", b=blocks, u=2)
+            src = hT[:].rearrange("p b u s -> p b s u")
+            if i in VCOPY:
+                nc.vector.tensor_copy(dst, src)
+            else:
+                nc.scalar.copy(dst, src)
+            nc.vector.quantize_mx(
+                out=codes[e][:, at : at + size].bitcast(FP8X4), scales=cs[e][:, at : at + size], in_=hq[:]
+            )
+            acc = psum_y.tile([P, size], F32, name="acc", tag="y")
+            second_layer(acc[:], e, 0, at, size)
+            nc.scalar.copy(y[0][:, lo : lo + size], acc[:])
+
+        gather(0)
+        for i in range(len(CHUNKS)):
+            if i + 1 < len(CHUNKS):
+                gather(i + 1)
+            hidden(i)
+
+        for n in range(1, NB):
+            for pair in range(E // 2):
+                acc = psum_y.tile([P, 2 * C], F32, name="acc", tag="y")
+                for j in range(2):
+                    second_layer(acc[:, j * C : (j + 1) * C], 2 * pair + j, n, 0, C)
+                nc.scalar.copy(y[n][:, pair * 2 * C : (pair + 1) * 2 * C], acc[:])
+
+        HALF = T // 2
+        for n in range(NB):
+            rows = slice(n * P, (n + 1) * P)
+            if n < NB - 1:
+                a = [deep.tile([P, T], F32, name=f"a{r}") for r in range(2)]
+                for r in range(2):
+                    nc.vector.tensor_tensor(a[r][:], y[n][:].indirect(pos_t[r][:]), g[r][:], MULT)
+                res = deep.tile([P, T], F32, name="res")
+                if n < PE_ADD:
+                    for h in range(2):
+                        sumT = psum.tile([P, HALF], F32, name="sumT", tag="a")
+                        for j in range(HALF // P):
+                            cols = slice(h * HALF + j * P, h * HALF + (j + 1) * P)
+                            for r in range(2):
+                                nc.tensor.matmul(
+                                    sumT[:, j * P : (j + 1) * P], a[r][:, cols], ident[:],
+                                    start=(r == 0), stop=(r == 1), is_transpose=True,
+                                )
+                        turned = deep.tile([P, HALF], F32, name="turned")
+                        nc.scalar.copy(turned[:], sumT[:])
+                        back = psum.tile([P, HALF], F32, name="back", tag="b")
+                        for j in range(HALF // P):
+                            nc.tensor.transpose(back[:, j * P : (j + 1) * P], turned[:, j * P : (j + 1) * P], ident[:])
+                        nc.scalar.copy(res[:, h * HALF : (h + 1) * HALF], back[:])
+                else:
+                    nc.vector.tensor_tensor(res[:], a[0][:], a[1][:], ADD)
+                nc.sync.dma_start(out[rows, :], res[:])
+            else:
+                for h in range(2):
+                    cols = slice(h * HALF, (h + 1) * HALF)
+                    a = [deep.tile([P, HALF], F32, name=f"last{r}") for r in range(2)]
+                    for r in range(2):
+                        nc.vector.tensor_tensor(
+                            a[r][:], y[n][:].indirect(pos_t[r][:, h * HALF // 16 : (h + 1) * HALF // 16]), g[r][:, cols], MULT
+                        )
+                    res = ring.tile([P, HALF], F32, name="res_last")
+                    nc.vector.tensor_tensor(res[:], a[0][:], a[1][:], ADD)
+                    nc.sync.dma_start(out[rows, cols], res[:])

@@ -25,7 +25,7 @@ SILU = mybir.ActivationFunctionType.Silu
 PACK = False
 PE_ADD = 7
 CHUNKS = [(0, 256), (256, 256), (512, 256), (768, 128), (896, 128)]
-VCOPY = ()
+VCOPY = (3, 4)
 
 
 def tile_moe_cpy_mlp_silu_kernel(
@@ -37,15 +37,16 @@ def tile_moe_cpy_mlp_silu_kernel(
         keep = ctx.enter_context(tc.tile_pool(name="keep", bufs=1))
         ring = ctx.enter_context(tc.tile_pool(name="ring", bufs=2))
         deep = ctx.enter_context(tc.tile_pool(name="deep", bufs=4))
-        psum = ctx.enter_context(tc.psum_pool(name="psum", bufs=2))
-        psum_y = ctx.enter_context(tc.psum_pool(name="psum_y", bufs=4))
+        psum = ctx.enter_context(tc.psum_pool(name="psum", bufs=3))
+        psum_y = ctx.enter_context(tc.psum_pool(name="psum_y", bufs=2))
 
         offs_t = lists.tile([P, S // 16], U16, name="offs_t")
         pos_t = [lists.tile([P, T // 16], U16, name=f"pos_t{r}") for r in range(2)]
 
         xw = [keep.tile([P, T], I32, name=f"xw{s}", align_bytes=64) for s in range(2)]
         xs = keep.tile([P, T if PACK else 2 * T], U8, name="xs", align_bytes=64)
-        w1 = [keep.tile([P, 2 * 2 * H], U8, name=f"w1_{e}", align_bytes=64) for e in range(E)]
+        w1p = [keep.tile([P, 8 * H], U8, name=f"w1_{e}", align_bytes=64) for e in range(2)]
+        w1 = [w1p[e // 2][:, (e % 2) * 4 * H : (e % 2 + 1) * 4 * H] for e in range(E)]
         w1s = keep.tile([P, E * 2 * H], U8, name="w1s", align_bytes=64)
         w2 = [keep.tile([P, E * K], U8, name=f"w2_{h}", align_bytes=64) for h in range(2)]
         w2s = keep.tile([P, E * K], U8, name="w2s", align_bytes=64)
@@ -57,18 +58,19 @@ def tile_moe_cpy_mlp_silu_kernel(
         nc.gpsimd.memset(xs[:].bitcast(I32), 0)
         nc.vector.memset(w1s[:].bitcast(I32), 0)
         nc.vector.memset(w2s[:].bitcast(I32), 0)
-        make_identity(nc, ident[:])
         for n in range(NB):
-            nc.gpsimd.memset(y[n][:, S + T : W], 0.0)
+            nc.vector.memset(y[n][:, S + T : W], 0.0)
 
-        SQ = nc.scalar
+        SQ = nc.sync
         nc.sync.dma_start(offs_t[:], offs)
+        nc.sync.dma_start(pos_t[0][:], pos1)
+        nc.sync.dma_start(pos_t[1][:], pos2)
         xs_d = x_scales.bitcast(I32)
         for q in range(4):
             if PACK:
-                SQ.dma_start(xs[32 * q : 32 * q + 8, :].bitcast(I32), xs_d[:, 4 * q : 4 * q + 4, :])
+                nc.scalar.dma_start(xs[32 * q : 32 * q + 8, :].bitcast(I32), xs_d[:, 4 * q : 4 * q + 4, :])
             else:
-                SQ.dma_start(
+                nc.scalar.dma_start(
                     xs[32 * q : 32 * q + 4, :].bitcast(I32).rearrange("r (s t) -> r s t", s=2),
                     xs_d[:, 4 * q : 4 * q + 4, :].rearrange("s r t -> r s t"),
                 )
@@ -80,12 +82,13 @@ def tile_moe_cpy_mlp_silu_kernel(
                 w1s[32 * q : 32 * q + 4, :].bitcast(I32).rearrange("r (a i) -> r a i", a=2 * E),
                 w1s_d[4 * q : 4 * q + 4],
             )
-        for e in range(E):
-            nc.sync.dma_start(
-                w1[e][:].bitcast(I32).rearrange("p (s i) -> p s i", s=2),
-                w1_words[e].bitcast(I32).rearrange("s p i -> p s i"),
+        for e in range(2):
+            nc.gpsimd.dma_start(
+                w1p[e][:].bitcast(I32).rearrange("p (a i) -> p a i", a=4),
+                w1_words[2 * e : 2 * e + 2].bitcast(I32).rearrange("e s p i -> p (e s) i"),
             )
-        nc.scalar.activation(warm[:], ident[:, 0:8], SILU)
+        make_identity(nc, ident[:])
+        nc.scalar.activation(warm[:], y[0][:, S + T : S + T + 8], SILU)
         w2s_d = w2_scales.bitcast(I32).rearrange("e s b n -> b (e s) n")
         for q in range(4):
             SQ.dma_start(
@@ -95,20 +98,18 @@ def tile_moe_cpy_mlp_silu_kernel(
         w2_d = w2_words.bitcast(I32).rearrange("e s p n -> p (e s) n")
 
         def load_w2(h):
-            nc.sync.dma_start(
+            nc.gpsimd.dma_start(
                 w2[h][:].bitcast(I32).rearrange("p (e n) -> p e n", e=E),
                 w2_d[:, :, h * (K // 4) : (h + 1) * (K // 4)],
             )
 
         def load_xr(n):
-            nc.sync.dma_start(y[n][:, S : S + T], xr[n * P : (n + 1) * P, :])
+            nc.gpsimd.dma_start(y[n][:, S : S + T], xr[n * P : (n + 1) * P, :])
 
         load_w2(0)
-        nc.sync.dma_start(pos_t[0][:], pos1)
-        nc.sync.dma_start(pos_t[1][:], pos2)
-        nc.sync.dma_start(g[0][:], gate[0])
+        nc.gpsimd.dma_start(g[0][:], gate[0])
         load_xr(0)
-        nc.sync.dma_start(g[1][:], gate[1])
+        nc.gpsimd.dma_start(g[1][:], gate[1])
         load_xr(1)
         load_w2(1)
         for n in range(2, NB):
@@ -210,48 +211,54 @@ def tile_moe_cpy_mlp_silu_kernel(
                 gather(i + 1)
             hidden(i)
 
-        for n in range(1, NB):
+        def slots_of(n):
             for pair in range(E // 2):
                 acc = psum_y.tile([P, 2 * C], F32, name="acc", tag="y")
                 for j in range(2):
                     second_layer(acc[:, j * C : (j + 1) * C], 2 * pair + j, n, 0, C)
                 nc.scalar.copy(y[n][:, pair * 2 * C : (pair + 1) * 2 * C], acc[:])
 
-        HALF = T // 2
+
+        def weighted(n, lo, size):
+            a = [deep.tile([P, size], F32, name=f"a{r}") for r in range(2)]
+            for r in range(2):
+                nc.vector.tensor_tensor(
+                    a[r][:], y[n][:].indirect(pos_t[r][:, lo // 16 : (lo + size) // 16]), g[r][:, lo : lo + size], MULT
+                )
+            return a
+
+        def add_on_tensor(a, at, size, res):
+            sumT = psum.tile([P, size], F32, name="sumT", tag="a")
+            for j in range(size // P):
+                for r in range(2):
+                    nc.tensor.matmul(
+                        sumT[:, j * P : (j + 1) * P], a[r][:, at + j * P : at + (j + 1) * P], ident[:],
+                        start=(r == 0), stop=(r == 1), is_transpose=True,
+                    )
+            turned = deep.tile([P, size], F32, name="turned")
+            nc.scalar.copy(turned[:], sumT[:])
+            back = psum.tile([P, size], F32, name="back", tag="b")
+            for j in range(size // P):
+                nc.tensor.transpose(back[:, j * P : (j + 1) * P], turned[:, j * P : (j + 1) * P], ident[:])
+            nc.scalar.copy(res[:, at : at + size], back[:])
+
+        PLAN = [[(-768,)]] * 7 + [[(-384,), (-384,)]]
+        slots_of(1)
         for n in range(NB):
             rows = slice(n * P, (n + 1) * P)
-            if n < NB - 1:
-                a = [deep.tile([P, T], F32, name=f"a{r}") for r in range(2)]
-                for r in range(2):
-                    nc.vector.tensor_tensor(a[r][:], y[n][:].indirect(pos_t[r][:]), g[r][:], MULT)
-                res = deep.tile([P, T], F32, name="res")
-                if n < PE_ADD:
-                    for h in range(2):
-                        sumT = psum.tile([P, HALF], F32, name="sumT", tag="a")
-                        for j in range(HALF // P):
-                            cols = slice(h * HALF + j * P, h * HALF + (j + 1) * P)
-                            for r in range(2):
-                                nc.tensor.matmul(
-                                    sumT[:, j * P : (j + 1) * P], a[r][:, cols], ident[:],
-                                    start=(r == 0), stop=(r == 1), is_transpose=True,
-                                )
-                        turned = deep.tile([P, HALF], F32, name="turned")
-                        nc.scalar.copy(turned[:], sumT[:])
-                        back = psum.tile([P, HALF], F32, name="back", tag="b")
-                        for j in range(HALF // P):
-                            nc.tensor.transpose(back[:, j * P : (j + 1) * P], turned[:, j * P : (j + 1) * P], ident[:])
-                        nc.scalar.copy(res[:, h * HALF : (h + 1) * HALF], back[:])
-                else:
-                    nc.vector.tensor_tensor(res[:], a[0][:], a[1][:], ADD)
-                nc.sync.dma_start(out[rows, :], res[:])
-            else:
-                for h in range(2):
-                    cols = slice(h * HALF, (h + 1) * HALF)
-                    a = [deep.tile([P, HALF], F32, name=f"last{r}") for r in range(2)]
-                    for r in range(2):
-                        nc.vector.tensor_tensor(
-                            a[r][:], y[n][:].indirect(pos_t[r][:, h * HALF // 16 : (h + 1) * HALF // 16]), g[r][:, cols], MULT
-                        )
-                    res = ring.tile([P, HALF], F32, name="res_last")
-                    nc.vector.tensor_tensor(res[:], a[0][:], a[1][:], ADD)
-                    nc.sync.dma_start(out[rows, cols], res[:])
+            lo = 0
+            for pieces in PLAN[n]:
+                size = sum(abs(x) for x in pieces)
+                a = weighted(n, lo, size)
+                res = deep.tile([P, size], F32, name="res")
+                at = 0
+                for x in pieces:
+                    if x > 0:
+                        add_on_tensor(a, at, x, res)
+                    else:
+                        nc.vector.tensor_tensor(res[:, at : at - x], a[0][:, at : at - x], a[1][:, at : at - x], ADD)
+                    at += abs(x)
+                nc.sync.dma_start(out[rows, lo : lo + size], res[:])
+                lo += size
+            if n + 2 < NB:
+                slots_of(n + 2)

@@ -22,10 +22,10 @@ MULT = mybir.AluOpType.mult
 ADD = mybir.AluOpType.add
 SILU = mybir.ActivationFunctionType.Silu
 
-PACK = False
+PACK = True
 PE_ADD = 7
 CHUNKS = [(0, 256), (256, 256), (512, 256), (768, 128), (896, 128)]
-VCOPY = (3, 4)
+VCOPY = (1, 2, 3, 4)
 
 
 def tile_moe_cpy_mlp_silu_kernel(
@@ -43,7 +43,7 @@ def tile_moe_cpy_mlp_silu_kernel(
         offs_t = lists.tile([P, S // 16], U16, name="offs_t")
         pos_t = [lists.tile([P, T // 16], U16, name=f"pos_t{r}") for r in range(2)]
 
-        xw = [keep.tile([P, T], I32, name=f"xw{s}", align_bytes=64) for s in range(2)]
+        xw = keep.tile([P, 2, T], I32, name="xw", align_bytes=64)
         xs = keep.tile([P, T if PACK else 2 * T], U8, name="xs", align_bytes=64)
         w1p = [keep.tile([P, 8 * H], U8, name=f"w1_{e}", align_bytes=64) for e in range(2)]
         w1 = [w1p[e // 2][:, (e % 2) * 4 * H : (e % 2 + 1) * 4 * H] for e in range(E)]
@@ -57,7 +57,6 @@ def tile_moe_cpy_mlp_silu_kernel(
 
         nc.gpsimd.memset(xs[:].bitcast(I32), 0)
         nc.vector.memset(w1s[:].bitcast(I32), 0)
-        nc.vector.memset(w2s[:].bitcast(I32), 0)
         for n in range(NB):
             nc.vector.memset(y[n][:, S + T : W], 0.0)
 
@@ -74,8 +73,7 @@ def tile_moe_cpy_mlp_silu_kernel(
                     xs[32 * q : 32 * q + 4, :].bitcast(I32).rearrange("r (s t) -> r s t", s=2),
                     xs_d[:, 4 * q : 4 * q + 4, :].rearrange("s r t -> r s t"),
                 )
-        for s in range(2):
-            nc.sync.dma_start(xw[s][:], x_words[s].rearrange("p t d -> p (t d)").bitcast(I32))
+        nc.sync.dma_start(xw[:], x_words.rearrange("s p t d -> p s (t d)").bitcast(I32))
         w1s_d = w1_scales.bitcast(I32).rearrange("e s b i -> b (e s) i")
         for q in range(4):
             SQ.dma_start(
@@ -88,6 +86,7 @@ def tile_moe_cpy_mlp_silu_kernel(
                 w1_words[2 * e : 2 * e + 2].bitcast(I32).rearrange("e s p i -> p (e s) i"),
             )
         make_identity(nc, ident[:])
+        nc.gpsimd.memset(w2s[:].bitcast(I32), 0)
         nc.scalar.activation(warm[:], y[0][:, S + T : S + T + 8], SILU)
         w2s_d = w2_scales.bitcast(I32).rearrange("e s b n -> b (e s) n")
         for q in range(4):
@@ -126,7 +125,7 @@ def tile_moe_cpy_mlp_silu_kernel(
                 both, moved = halves[a]
                 nc.vector.tensor_copy(both[:], xs[:].indirect(offs_t[:, a * 32 : (a + 1) * 32]))
                 for q in range(4):
-                    nc.scalar.dma_start(
+                    nc.sync.dma_start(
                         moved[32 * q : 32 * q + 4, :].bitcast(I32), both[32 * q + 4 : 32 * q + 8, :].bitcast(I32)
                     )
 
@@ -153,7 +152,7 @@ def tile_moe_cpy_mlp_silu_kernel(
             xg, sg = [], []
             for s in range(2):
                 w = keep.tile([P, size], U32, name=f"xg{i}_{s}", align_bytes=64)
-                nc.vector.tensor_copy(w[:], xw[s][:].bitcast(U32).indirect(idx))
+                nc.vector.tensor_copy(w[:], xw[:, s, :].bitcast(U32).indirect(idx))
                 xg.append(w[:])
                 if PACK:
                     a, at = divmod(lo, S // 2)
@@ -220,7 +219,7 @@ def tile_moe_cpy_mlp_silu_kernel(
 
 
         def weighted(n, lo, size):
-            a = [deep.tile([P, size], F32, name=f"a{r}") for r in range(2)]
+            a = [deep.tile([P, size], F32, name=f"a{r}", bufs=8) for r in range(2)]
             for r in range(2):
                 nc.vector.tensor_tensor(
                     a[r][:], y[n][:].indirect(pos_t[r][:, lo // 16 : (lo + size) // 16]), g[r][:, lo : lo + size], MULT
@@ -242,8 +241,9 @@ def tile_moe_cpy_mlp_silu_kernel(
                 nc.tensor.transpose(back[:, j * P : (j + 1) * P], turned[:, j * P : (j + 1) * P], ident[:])
             nc.scalar.copy(res[:, at : at + size], back[:])
 
-        PLAN = [[(-768,)]] * 7 + [[(-384,), (-384,)]]
-        slots_of(1)
+        PLAN = [[(384, 384)]] * 7 + [[(-512,), (-256,)]]
+        for n in range(1, NB):
+            slots_of(n)
         for n in range(NB):
             rows = slice(n * P, (n + 1) * P)
             lo = 0
@@ -257,8 +257,9 @@ def tile_moe_cpy_mlp_silu_kernel(
                         add_on_tensor(a, at, x, res)
                     else:
                         nc.vector.tensor_tensor(res[:, at : at - x], a[0][:, at : at - x], a[1][:, at : at - x], ADD)
+                    if n == NB - 2:
+                        nc.sync.dma_start(out[rows, lo + at : lo + at + abs(x)], res[:, at : at + abs(x)])
                     at += abs(x)
-                nc.sync.dma_start(out[rows, lo : lo + size], res[:])
+                if n != NB - 2:
+                    nc.sync.dma_start(out[rows, lo : lo + size], res[:])
                 lo += size
-            if n + 2 < NB:
-                slots_of(n + 2)

@@ -22,10 +22,9 @@ MULT = mybir.AluOpType.mult
 ADD = mybir.AluOpType.add
 SILU = mybir.ActivationFunctionType.Silu
 
-PACK = True
-PE_ADD = 7
-CHUNKS = [(0, 256), (256, 256), (512, 256), (768, 128), (896, 128)]
-VCOPY = (1, 2, 3, 4)
+SCALE_RUNS = [(0, C), (C, S - C)]
+WORD_RUNS = [(0, 128), (128, 128), (256, 256), (512, 256), (768, 128), (896, 128)]
+HALF = T // 2
 
 
 def tile_moe_cpy_mlp_silu_kernel(
@@ -35,8 +34,7 @@ def tile_moe_cpy_mlp_silu_kernel(
     with ExitStack() as ctx:
         lists = ctx.enter_context(tc.tile_pool(name="lists", bufs=1))
         keep = ctx.enter_context(tc.tile_pool(name="keep", bufs=1))
-        ring = ctx.enter_context(tc.tile_pool(name="ring", bufs=2))
-        deep = ctx.enter_context(tc.tile_pool(name="deep", bufs=4))
+        share = ctx.enter_context(tc.tile_pool(name="share", bufs=1))
         psum = ctx.enter_context(tc.psum_pool(name="psum", bufs=3))
         psum_y = ctx.enter_context(tc.psum_pool(name="psum_y", bufs=2))
 
@@ -44,56 +42,41 @@ def tile_moe_cpy_mlp_silu_kernel(
         pos_t = [lists.tile([P, T // 16], U16, name=f"pos_t{r}") for r in range(2)]
 
         xw = keep.tile([P, 2, T], I32, name="xw", align_bytes=64)
-        xs = keep.tile([P, T if PACK else 2 * T], U8, name="xs", align_bytes=64)
+        xs = share.tile([P, T], U8, name="xs", offset=8 * S - T // 2, align_bytes=64)
         w1p = [keep.tile([P, 8 * H], U8, name=f"w1_{e}", align_bytes=64) for e in range(2)]
         w1 = [w1p[e // 2][:, (e % 2) * 4 * H : (e % 2 + 1) * 4 * H] for e in range(E)]
         w1s = keep.tile([P, E * 2 * H], U8, name="w1s", align_bytes=64)
         w2 = [keep.tile([P, E * K], U8, name=f"w2_{h}", align_bytes=64) for h in range(2)]
         w2s = keep.tile([P, E * K], U8, name="w2s", align_bytes=64)
-        g = [keep.tile([P, T], F32, name=f"g{r}") for r in range(2)]
         y = [keep.tile([P, W], F32, name=f"y{n}") for n in range(NB)]
         ident = keep.tile([P, P], F32, name="ident")
         warm = keep.tile([P, 8], F32, name="warm")
+        both = [keep.tile([P, size], U8, name=f"both{lo}", align_bytes=64) for lo, size in SCALE_RUNS]
+        moved = [keep.tile([P, size], U8, name=f"moved{lo}", align_bytes=64) for lo, size in SCALE_RUNS]
 
-        nc.gpsimd.memset(xs[:].bitcast(I32), 0)
+        nc.vector.memset(xs[:].bitcast(I32), 0)
         nc.vector.memset(w1s[:].bitcast(I32), 0)
-        for n in range(NB):
-            nc.vector.memset(y[n][:, S + T : W], 0.0)
+        nc.vector.memset(ident[:], 0.0)
+        for tile in moved:
+            nc.vector.memset(tile[:].bitcast(I32), 0)
+        nc.vector.memset(y[0][:, S + T : W], 0.0)
 
-        SQ = nc.sync
         nc.sync.dma_start(offs_t[:], offs)
-        nc.sync.dma_start(pos_t[0][:], pos1)
-        nc.sync.dma_start(pos_t[1][:], pos2)
         xs_d = x_scales.bitcast(I32)
         for q in range(4):
-            if PACK:
-                nc.scalar.dma_start(xs[32 * q : 32 * q + 8, :].bitcast(I32), xs_d[:, 4 * q : 4 * q + 4, :])
-            else:
-                nc.scalar.dma_start(
-                    xs[32 * q : 32 * q + 4, :].bitcast(I32).rearrange("r (s t) -> r s t", s=2),
-                    xs_d[:, 4 * q : 4 * q + 4, :].rearrange("s r t -> r s t"),
-                )
-        nc.sync.dma_start(xw[:], x_words.rearrange("s p t d -> p s (t d)").bitcast(I32))
+            nc.sync.dma_start(xs[32 * q : 32 * q + 8, :].bitcast(I32), xs_d[:, 4 * q : 4 * q + 4, :])
+        nc.gpsimd.dma_start(xw[:], x_words.rearrange("s p t d -> p s (t d)").bitcast(I32))
+        nc.scalar.activation(warm[:], ident[:, 0:8], SILU)
+        for n in range(1, NB):
+            nc.scalar.copy(y[n][:, S + T : W], y[0][:, S + T : W])
         w1s_d = w1_scales.bitcast(I32).rearrange("e s b i -> b (e s) i")
         for q in range(4):
-            SQ.dma_start(
+            nc.sync.dma_start(
                 w1s[32 * q : 32 * q + 4, :].bitcast(I32).rearrange("r (a i) -> r a i", a=2 * E),
                 w1s_d[4 * q : 4 * q + 4],
             )
-        for e in range(2):
-            nc.gpsimd.dma_start(
-                w1p[e][:].bitcast(I32).rearrange("p (a i) -> p a i", a=4),
-                w1_words[2 * e : 2 * e + 2].bitcast(I32).rearrange("e s p i -> p (e s) i"),
-            )
-        make_identity(nc, ident[:])
-        nc.gpsimd.memset(w2s[:].bitcast(I32), 0)
-        nc.scalar.activation(warm[:], y[0][:, S + T : S + T + 8], SILU)
-        w2s_d = w2_scales.bitcast(I32).rearrange("e s b n -> b (e s) n")
-        for q in range(4):
-            SQ.dma_start(
-                w2s[32 * q : 32 * q + 4, :].bitcast(I32).rearrange("r (e n) -> r e n", e=E),
-                w2s_d[4 * q : 4 * q + 4],
-            )
+        nc.sync.dma_start(pos_t[0][:], pos1)
+        nc.sync.dma_start(pos_t[1][:], pos2)
         w2_d = w2_words.bitcast(I32).rearrange("e s p n -> p (e s) n")
 
         def load_w2(h):
@@ -105,161 +88,200 @@ def tile_moe_cpy_mlp_silu_kernel(
         def load_xr(n):
             nc.gpsimd.dma_start(y[n][:, S : S + T], xr[n * P : (n + 1) * P, :])
 
+        def load_w1(h):
+            nc.gpsimd.dma_start(
+                w1p[h][:].bitcast(I32).rearrange("p (a i) -> p a i", a=4),
+                w1_words[2 * h : 2 * h + 2].bitcast(I32).rearrange("e s p i -> p (e s) i"),
+            )
+
+        load_w1(0)
+        make_identity(nc, ident[:], nomemset=True)
+        nc.gpsimd.memset(w2s[:].bitcast(I32), 0)
+        load_w1(1)
+
+        for a, (lo, size) in enumerate(SCALE_RUNS):
+            for at in range(0, size, 2 * C):
+                run = min(2 * C, size - at)
+                nc.vector.tensor_copy(
+                    both[a][:, at : at + run], xs[:].indirect(offs_t[:, (lo + at) // 16 : (lo + at + run) // 16])
+                )
+            for q in range(4):
+                nc.scalar.dma_start(
+                    moved[a][32 * q : 32 * q + 4, :].bitcast(I32), both[a][32 * q + 4 : 32 * q + 8, :].bitcast(I32)
+                )
+
+        w2s_d = w2_scales.bitcast(I32).rearrange("e s b n -> b (e s) n")
+        for q in range(4):
+            nc.sync.dma_start(
+                w2s[32 * q : 32 * q + 4, :].bitcast(I32).rearrange("r (e n) -> r e n", e=E),
+                w2s_d[4 * q : 4 * q + 4],
+            )
+
+        g = share.tile([P, 2, T], F32, name="g", offset=8 * S, align_bytes=64)
+        nc.gpsimd.dma_start(g[:], gate.rearrange("r p t -> p r t"))
         load_w2(0)
-        nc.gpsimd.dma_start(g[0][:], gate[0])
         load_xr(0)
-        nc.gpsimd.dma_start(g[1][:], gate[1])
         load_xr(1)
         load_w2(1)
         for n in range(2, NB):
             load_xr(n)
 
-        if PACK:
-            halves = []
-            for a in range(2):
-                both = keep.tile([P, S // 2], U8, name=f"both{a}", align_bytes=64)
-                moved = keep.tile([P, S // 2], U8, name=f"moved{a}", align_bytes=64)
-                nc.vector.memset(moved[:].bitcast(I32), 0)
-                halves.append((both, moved))
-            for a in range(2):
-                both, moved = halves[a]
-                nc.vector.tensor_copy(both[:], xs[:].indirect(offs_t[:, a * 32 : (a + 1) * 32]))
-                for q in range(4):
-                    nc.sync.dma_start(
-                        moved[32 * q : 32 * q + 4, :].bitcast(I32), both[32 * q + 4 : 32 * q + 8, :].bitcast(I32)
-                    )
+        words = share.tile([P, 2 * S], U32, name="words", offset=0, align_bytes=64)
+        for lo, size in WORD_RUNS:
+            for s in range(2):
+                nc.vector.tensor_copy(
+                    words[:, s * S + lo : s * S + lo + size],
+                    xw[:, s, :].bitcast(U32).indirect(offs_t[:, lo // 16 : (lo + size) // 16]),
+                )
+
+        def slot_scales(lo, s):
+            a = 0 if lo < C else 1
+            at = lo - SCALE_RUNS[a][0]
+            return (both, moved)[s][a][:, at : at + P]
 
         codes = [keep.tile([P, C], U32, name=f"codes{e}", align_bytes=64) for e in range(E)]
         cs = [keep.tile([P, C], U8, name=f"cs{e}", align_bytes=64) for e in range(E)]
 
-        def second_layer(acc, e, n, lo, size):
-            h, m = divmod(n, NB // 2)
-            nc.tensor.matmul_mx(
-                out=acc,
-                lhsT=w2[h][:, e * K + m * 2 * P : e * K + (m + 1) * 2 * P].bitcast(FP4X4),
-                lhsT_scale=w2s[:, e * K + n * P : e * K + (n + 1) * P],
-                rhs=codes[e][:, lo : lo + size].bitcast(FP8X4),
-                rhs_scale=cs[e][:, lo : lo + size],
-                start=True,
-                stop=True,
+        hb = {}
+
+        def first_layer(lo):
+            e = lo // C
+            pre = psum.tile([P, H], F32, name="pre", tag="a")
+            for s in range(2):
+                nc.tensor.matmul_mx(
+                    out=pre[:],
+                    lhsT=words[:, s * S + lo : s * S + lo + P].bitcast(FP8X4),
+                    lhsT_scale=slot_scales(lo, s),
+                    rhs=w1[e][:, s * 2 * H : (s + 1) * 2 * H].bitcast(FP4X4),
+                    rhs_scale=w1s[:, (2 * e + s) * H : (2 * e + s + 1) * H],
+                    start=(s == 0),
+                    stop=(s == 1),
+                )
+            hb[lo] = keep.tile([P, H], BF16, name=f"hb{lo}")
+            nc.scalar.activation(
+                hb[lo][:].rearrange("s (u p d) -> s u p d", u=2, d=2),
+                pre[:].rearrange("s (p u d) -> s u p d", u=2, d=2),
+                SILU,
             )
 
-        gathered = {}
+        hq = [keep.tile([P, 4 * C], BF16, name=f"hq{e}", align_bytes=64) for e in range(E)]
 
-        def gather(i):
-            lo, size = CHUNKS[i]
-            idx = offs_t[:, lo // 16 : (lo + size) // 16]
-            xg, sg = [], []
-            for s in range(2):
-                w = keep.tile([P, size], U32, name=f"xg{i}_{s}", align_bytes=64)
-                nc.vector.tensor_copy(w[:], xw[:, s, :].bitcast(U32).indirect(idx))
-                xg.append(w[:])
-                if PACK:
-                    a, at = divmod(lo, S // 2)
-                    sg.append(halves[a][s][:, at : at + size])
-                else:
-                    b = keep.tile([P, size], U8, name=f"sg{i}_{s}", align_bytes=64)
-                    nc.vector.tensor_copy(b[:], xs[:, s * T : (s + 1) * T].indirect(idx))
-                    sg.append(b[:])
-            gathered[i] = (xg, sg)
-
-        def hidden(i):
-            lo, size = CHUNKS[i]
+        def turn(lo, size, copy):
             e, at = divmod(lo, C)
-            xg, sg = gathered[i]
             blocks = size // P
             hT = psum.tile([P, blocks, 2, P], F32, name="hT", tag="b")
             for b in range(blocks):
-                pre = psum.tile([P, H], F32, name="pre", tag="a")
-                for s in range(2):
-                    nc.tensor.matmul_mx(
-                        out=pre[:],
-                        lhsT=xg[s][:, b * P : (b + 1) * P].bitcast(FP8X4),
-                        lhsT_scale=sg[s][:, b * P : (b + 1) * P],
-                        rhs=w1[e][:, s * 2 * H : (s + 1) * 2 * H].bitcast(FP4X4),
-                        rhs_scale=w1s[:, (2 * e + s) * H : (2 * e + s + 1) * H],
-                        start=(s == 0),
-                        stop=(s == 1),
-                    )
-                hb = ring.tile([P, H], BF16, name="hb")
-                nc.scalar.activation(
-                    hb[:].rearrange("s (u p d) -> s u p d", u=2, d=2),
-                    pre[:].rearrange("s (p u d) -> s u p d", u=2, d=2),
-                    SILU,
-                )
-                words = hb[:].bitcast(F32)
+                pairs = hb[lo + b * P][:].bitcast(F32)
                 for u in range(2):
-                    nc.tensor.transpose(hT[:, b, u, :], words[:, u * P : (u + 1) * P], ident[:])
-            hq = ring.tile([P, 4 * size], BF16, name="hq", align_bytes=64)
-            dst = hq[:].bitcast(F32).rearrange("p (b s u) -> p b s u", b=blocks, u=2)
-            src = hT[:].rearrange("p b u s -> p b s u")
-            if i in VCOPY:
-                nc.vector.tensor_copy(dst, src)
-            else:
-                nc.scalar.copy(dst, src)
-            nc.vector.quantize_mx(
-                out=codes[e][:, at : at + size].bitcast(FP8X4), scales=cs[e][:, at : at + size], in_=hq[:]
+                    nc.tensor.transpose(hT[:, b, u, :], pairs[:, u * P : (u + 1) * P], ident[:])
+            copy(
+                hq[e][:, 4 * at : 4 * (at + size)].bitcast(F32).rearrange("p (b s u) -> p b s u", b=blocks, u=2),
+                hT[:].rearrange("p b u s -> p b s u"),
             )
-            acc = psum_y.tile([P, size], F32, name="acc", tag="y")
-            second_layer(acc[:], e, 0, at, size)
-            nc.scalar.copy(y[0][:, lo : lo + size], acc[:])
 
-        gather(0)
-        for i in range(len(CHUNKS)):
-            if i + 1 < len(CHUNKS):
-                gather(i + 1)
-            hidden(i)
+        def quantise(e):
+            nc.vector.quantize_mx(out=codes[e][:].bitcast(FP8X4), scales=cs[e][:], in_=hq[e][:])
+
+        for lo in range(0, 2 * C, P):
+            first_layer(lo)
+        turn(0, C, nc.scalar.copy)
+        quantise(0)
+        for lo in range(2 * C, 3 * C, P):
+            first_layer(lo)
+        turn(C, C, nc.vector.tensor_copy)
+        quantise(1)
+        for lo in range(3 * C, S, P):
+            first_layer(lo)
+        turn(2 * C, C, nc.vector.tensor_copy)
+        turn(3 * C, P, nc.vector.tensor_copy)
+        quantise(2)
+        turn(3 * C + P, P, nc.scalar.copy)
+        quantise(3)
+
+        def second_layer(acc, n, lo, size):
+            h, m = divmod(n, NB // 2)
+            done = 0
+            while done < size:
+                e, at = divmod(lo + done, C)
+                run = min(C - at, size - done)
+                nc.tensor.matmul_mx(
+                    out=acc[:, done : done + run],
+                    lhsT=w2[h][:, e * K + m * 2 * P : e * K + (m + 1) * 2 * P].bitcast(FP4X4),
+                    lhsT_scale=w2s[:, e * K + n * P : e * K + (n + 1) * P],
+                    rhs=codes[e][:, at : at + run].bitcast(FP8X4),
+                    rhs_scale=cs[e][:, at : at + run],
+                    start=True,
+                    stop=True,
+                )
+                done = done + run
+
+        acc = psum.tile([P, 2 * C], F32, name="acc_first", tag="a")
+        second_layer(acc, 0, 0, 2 * C)
+        nc.scalar.copy(y[0][:, 0 : 2 * C], acc[:])
+        acc = psum_y.tile([P, C], F32, name="acc", tag="y")
+        second_layer(acc, 0, 2 * C, C)
+        nc.vector.tensor_copy(y[0][:, 2 * C : 3 * C], acc[:])
+        acc = psum_y.tile([P, C], F32, name="acc", tag="y")
+        second_layer(acc, 0, 3 * C, C)
+        nc.scalar.copy(y[0][:, 3 * C : S], acc[:])
 
         def slots_of(n):
-            for pair in range(E // 2):
+            for lo in range(0, S, 2 * C):
                 acc = psum_y.tile([P, 2 * C], F32, name="acc", tag="y")
-                for j in range(2):
-                    second_layer(acc[:, j * C : (j + 1) * C], 2 * pair + j, n, 0, C)
-                nc.scalar.copy(y[n][:, pair * 2 * C : (pair + 1) * 2 * C], acc[:])
+                second_layer(acc, n, lo, 2 * C)
+                nc.scalar.copy(y[n][:, lo : lo + 2 * C], acc[:])
 
-
-        def weighted(n, lo, size):
-            a = [deep.tile([P, size], F32, name=f"a{r}", bufs=8) for r in range(2)]
-            for r in range(2):
-                nc.vector.tensor_tensor(
-                    a[r][:], y[n][:].indirect(pos_t[r][:, lo // 16 : (lo + size) // 16]), g[r][:, lo : lo + size], MULT
-                )
+        def weighted(n, r, lo, size):
+            a = keep.tile([P, size], F32, name=f"a{n}_{r}_{lo}")
+            nc.vector.tensor_tensor(
+                a[:], y[n][:].indirect(pos_t[r][:, lo // 16 : (lo + size) // 16]), g[:, r, lo : lo + size], MULT
+            )
             return a
 
-        def add_on_tensor(a, at, size, res):
-            sumT = psum.tile([P, size], F32, name="sumT", tag="a")
-            for j in range(size // P):
-                for r in range(2):
-                    nc.tensor.matmul(
-                        sumT[:, j * P : (j + 1) * P], a[r][:, at + j * P : at + (j + 1) * P], ident[:],
-                        start=(r == 0), stop=(r == 1), is_transpose=True,
-                    )
-            turned = deep.tile([P, size], F32, name="turned")
-            nc.scalar.copy(turned[:], sumT[:])
-            back = psum.tile([P, size], F32, name="back", tag="b")
-            for j in range(size // P):
-                nc.tensor.transpose(back[:, j * P : (j + 1) * P], turned[:, j * P : (j + 1) * P], ident[:])
-            nc.scalar.copy(res[:, at : at + size], back[:])
+        def turn_and_add(n):
+            a = [weighted(n, r, 0, T) for r in range(2)]
+            turned = []
+            for at in range(0, T, HALF):
+                sumT = psum.tile([P, HALF], F32, name="sumT", tag="a")
+                for j in range(0, HALF, P):
+                    for r in range(2):
+                        nc.tensor.matmul(
+                            sumT[:, j : j + P], a[r][:, at + j : at + j + P], ident[:],
+                            start=(r == 0), stop=(r == 1), is_transpose=True,
+                        )
+                if n == NB - 2:
+                    t = keep.tile([P, HALF], F32, name="turned", tag=f"last{at}")
+                else:
+                    t = keep.tile([P, HALF], F32, name="turned", bufs=4)
+                nc.scalar.copy(t[:], sumT[:])
+                turned.append(t)
+            return turned
 
-        PLAN = [[(384, 384)]] * 7 + [[(-512,), (-256,)]]
-        for n in range(1, NB):
+        def turn_back(n, turned):
+            res = keep.tile([P, T], F32, name="res", bufs=4)
+            for i, t in enumerate(turned):
+                back = psum.tile([P, HALF], F32, name="back", tag="b")
+                for j in range(0, HALF, P):
+                    nc.tensor.transpose(back[:, j : j + P], t[:, j : j + P], ident[:])
+                nc.scalar.copy(res[:, i * HALF : (i + 1) * HALF], back[:])
+                if n == NB - 2:
+                    nc.sync.dma_start(out[n * P : (n + 1) * P, i * HALF : (i + 1) * HALF], res[:, i * HALF : (i + 1) * HALF])
+            if n != NB - 2:
+                nc.sync.dma_start(out[n * P : (n + 1) * P, :], res[:])
+
+        for n in range(1, 4):
             slots_of(n)
-        for n in range(NB):
-            rows = slice(n * P, (n + 1) * P)
-            lo = 0
-            for pieces in PLAN[n]:
-                size = sum(abs(x) for x in pieces)
-                a = weighted(n, lo, size)
-                res = deep.tile([P, size], F32, name="res")
-                at = 0
-                for x in pieces:
-                    if x > 0:
-                        add_on_tensor(a, at, x, res)
-                    else:
-                        nc.vector.tensor_tensor(res[:, at : at - x], a[0][:, at : at - x], a[1][:, at : at - x], ADD)
-                    if n == NB - 2:
-                        nc.sync.dma_start(out[rows, lo + at : lo + at + abs(x)], res[:, at : at + abs(x)])
-                    at += abs(x)
-                if n != NB - 2:
-                    nc.sync.dma_start(out[rows, lo : lo + size], res[:])
-                lo += size
+        for n in range(NB - 1):
+            turned = turn_and_add(n)
+            if 4 + 2 * n < NB:
+                slots_of(4 + 2 * n)
+            turn_back(n, turned)
+            if 5 + 2 * n < NB:
+                slots_of(5 + 2 * n)
+
+        n = NB - 1
+        a = [weighted(n, r, 0, T) for r in range(2)]
+        for at in range(0, T, HALF):
+            res = keep.tile([P, HALF], F32, name="res_last", tag=f"last{at}")
+            nc.vector.tensor_tensor(res[:], a[0][:, at : at + HALF], a[1][:, at : at + HALF], ADD)
+            nc.sync.dma_start(out[n * P : (n + 1) * P, at : at + HALF], res[:])

@@ -35,13 +35,13 @@ def tile_moe_cpy_mlp_silu_kernel(
         lists = ctx.enter_context(tc.tile_pool(name="lists", bufs=1))
         keep = ctx.enter_context(tc.tile_pool(name="keep", bufs=1))
         share = ctx.enter_context(tc.tile_pool(name="share", bufs=1))
-        psum = ctx.enter_context(tc.psum_pool(name="psum", bufs=3))
+        psum = ctx.enter_context(tc.psum_pool(name="psum", bufs=2))
         psum_y = ctx.enter_context(tc.psum_pool(name="psum_y", bufs=2))
 
         offs_t = lists.tile([P, S // 16], U16, name="offs_t")
         pos_t = [lists.tile([P, T // 16], U16, name=f"pos_t{r}") for r in range(2)]
 
-        xw = keep.tile([P, 2, T], I32, name="xw", align_bytes=64)
+        xw = [keep.tile([P, T], I32, name=f"xw{s}", align_bytes=64) for s in range(2)]
         xs = share.tile([P, T], U8, name="xs", offset=8 * S - T // 2, align_bytes=64)
         w1p = [keep.tile([P, 8 * H], U8, name=f"w1_{e}", align_bytes=64) for e in range(2)]
         w1 = [w1p[e // 2][:, (e % 2) * 4 * H : (e % 2 + 1) * 4 * H] for e in range(E)]
@@ -61,19 +61,20 @@ def tile_moe_cpy_mlp_silu_kernel(
             nc.vector.memset(tile[:].bitcast(I32), 0)
         nc.vector.memset(y[0][:, S + T : W], 0.0)
 
+        xw_d = x_words.rearrange("s p t d -> s p (t d)").bitcast(I32)
         nc.sync.dma_start(offs_t[:], offs)
+        nc.scalar.dma_start(xw[0][:], xw_d[0])
         xs_d = x_scales.bitcast(I32)
         for q in range(4):
             nc.sync.dma_start(xs[32 * q : 32 * q + 8, :].bitcast(I32), xs_d[:, 4 * q : 4 * q + 4, :])
-        nc.gpsimd.dma_start(xw[:], x_words.rearrange("s p t d -> p s (t d)").bitcast(I32))
         nc.scalar.activation(warm[:], ident[:, 0:8], SILU)
         for n in range(1, NB):
             nc.scalar.copy(y[n][:, S + T : W], y[0][:, S + T : W])
         w1s_d = w1_scales.bitcast(I32).rearrange("e s b i -> b (e s) i")
-        for q in range(4):
+        for r in range(4):
             nc.sync.dma_start(
-                w1s[32 * q : 32 * q + 4, :].bitcast(I32).rearrange("r (a i) -> r a i", a=2 * E),
-                w1s_d[4 * q : 4 * q + 4],
+                w1s[r:P:32, :].bitcast(I32).rearrange("q (a i) -> q a i", a=2 * E),
+                w1s_d[r:16:4],
             )
         nc.sync.dma_start(pos_t[0][:], pos1)
         nc.sync.dma_start(pos_t[1][:], pos2)
@@ -95,6 +96,7 @@ def tile_moe_cpy_mlp_silu_kernel(
             )
 
         load_w1(0)
+        nc.gpsimd.dma_start(xw[1][:], xw_d[1])
         make_identity(nc, ident[:], nomemset=True)
         nc.gpsimd.memset(w2s[:].bitcast(I32), 0)
         load_w1(1)
@@ -111,10 +113,10 @@ def tile_moe_cpy_mlp_silu_kernel(
                 )
 
         w2s_d = w2_scales.bitcast(I32).rearrange("e s b n -> b (e s) n")
-        for q in range(4):
+        for r in range(4):
             nc.sync.dma_start(
-                w2s[32 * q : 32 * q + 4, :].bitcast(I32).rearrange("r (e n) -> r e n", e=E),
-                w2s_d[4 * q : 4 * q + 4],
+                w2s[r:P:32, :].bitcast(I32).rearrange("q (e n) -> q e n", e=E),
+                w2s_d[r:16:4],
             )
 
         g = share.tile([P, 2, T], F32, name="g", offset=8 * S, align_bytes=64)
@@ -131,7 +133,7 @@ def tile_moe_cpy_mlp_silu_kernel(
             for s in range(2):
                 nc.vector.tensor_copy(
                     words[:, s * S + lo : s * S + lo + size],
-                    xw[:, s, :].bitcast(U32).indirect(offs_t[:, lo // 16 : (lo + size) // 16]),
+                    xw[s][:].bitcast(U32).indirect(offs_t[:, lo // 16 : (lo + size) // 16]),
                 )
 
         def slot_scales(lo, s):
@@ -146,7 +148,7 @@ def tile_moe_cpy_mlp_silu_kernel(
 
         def first_layer(lo):
             e = lo // C
-            pre = psum.tile([P, H], F32, name="pre", tag="a")
+            pre = psum.tile([P, H], F32, name="pre", tag="a", bufs=4)
             for s in range(2):
                 nc.tensor.matmul_mx(
                     out=pre[:],
@@ -179,24 +181,30 @@ def tile_moe_cpy_mlp_silu_kernel(
                 hT[:].rearrange("p b u s -> p b s u"),
             )
 
-        def quantise(e):
-            nc.vector.quantize_mx(out=codes[e][:].bitcast(FP8X4), scales=cs[e][:], in_=hq[e][:])
+        def quantise(lo, size):
+            e, at = divmod(lo, C)
+            nc.vector.quantize_mx(
+                out=codes[e][:, at : at + size].bitcast(FP8X4),
+                scales=cs[e][:, at : at + size],
+                in_=hq[e][:, 4 * at : 4 * (at + size)],
+            )
 
         for lo in range(0, 2 * C, P):
             first_layer(lo)
-        turn(0, C, nc.scalar.copy)
-        quantise(0)
+        turn(0, C, nc.vector.tensor_copy)
+        quantise(0, C)
         for lo in range(2 * C, 3 * C, P):
             first_layer(lo)
         turn(C, C, nc.vector.tensor_copy)
-        quantise(1)
+        quantise(C, C)
         for lo in range(3 * C, S, P):
             first_layer(lo)
         turn(2 * C, C, nc.vector.tensor_copy)
+        quantise(2 * C, C)
         turn(3 * C, P, nc.vector.tensor_copy)
-        quantise(2)
-        turn(3 * C + P, P, nc.scalar.copy)
-        quantise(3)
+        quantise(3 * C, P)
+        turn(S - P, P, nc.scalar.copy)
+        quantise(S - P, P)
 
         def second_layer(acc, n, lo, size):
             h, m = divmod(n, NB // 2)
@@ -215,15 +223,15 @@ def tile_moe_cpy_mlp_silu_kernel(
                 )
                 done = done + run
 
-        acc = psum.tile([P, 2 * C], F32, name="acc_first", tag="a")
+        acc = psum.tile([P, 2 * C], F32, name="acc_first", tag="a", bufs=4)
         second_layer(acc, 0, 0, 2 * C)
         nc.scalar.copy(y[0][:, 0 : 2 * C], acc[:])
-        acc = psum_y.tile([P, C], F32, name="acc", tag="y")
-        second_layer(acc, 0, 2 * C, C)
-        nc.vector.tensor_copy(y[0][:, 2 * C : 3 * C], acc[:])
-        acc = psum_y.tile([P, C], F32, name="acc", tag="y")
-        second_layer(acc, 0, 3 * C, C)
-        nc.scalar.copy(y[0][:, 3 * C : S], acc[:])
+        acc = psum_y.tile([P, C + P], F32, name="acc", tag="y")
+        second_layer(acc, 0, 2 * C, C + P)
+        nc.vector.tensor_copy(y[0][:, 2 * C : S - P], acc[:])
+        acc = psum_y.tile([P, P], F32, name="acc", tag="y")
+        second_layer(acc, 0, S - P, P)
+        nc.scalar.copy(y[0][:, S - P : S], acc[:])
 
         def slots_of(n):
             for lo in range(0, S, 2 * C):
@@ -242,7 +250,7 @@ def tile_moe_cpy_mlp_silu_kernel(
             a = [weighted(n, r, 0, T) for r in range(2)]
             turned = []
             for at in range(0, T, HALF):
-                sumT = psum.tile([P, HALF], F32, name="sumT", tag="a")
+                sumT = psum.tile([P, HALF], F32, name="sumT", tag="a", bufs=4)
                 for j in range(0, HALF, P):
                     for r in range(2):
                         nc.tensor.matmul(

@@ -22,9 +22,16 @@ MULT = mybir.AluOpType.mult
 ADD = mybir.AluOpType.add
 SILU = mybir.ActivationFunctionType.Silu
 
-SCALE_RUNS = [(0, C), (C, S - C)]
-WORD_RUNS = [(0, 128), (128, 128), (256, 256), (512, 256), (768, 128), (896, 128)]
 HALF = T // 2
+KB = 1024
+STAGES = [
+    (0, 512, 6 * KB, [(0, 128, 0), (128, 128, 2 * KB), (256, 256, 4 * KB)]),
+    (512, 256, 0, [(512, 128, KB + KB // 2), (640, 128, 2 * KB + KB // 2)]),
+    (768, 256, 4 * KB, [(768, 128, 5 * KB + KB // 2), (896, 128, 6 * KB + KB // 2)]),
+]
+XW_AT = 8 * KB
+W1_LOADS = [(0, 1), (1, 1), (2, 2)]
+GROUPS = [(0, 512), (512, 256), (768, 128), (896, 128)]
 
 
 def tile_moe_cpy_mlp_silu_kernel(
@@ -41,34 +48,32 @@ def tile_moe_cpy_mlp_silu_kernel(
         offs_t = lists.tile([P, S // 16], U16, name="offs_t")
         pos_t = [lists.tile([P, T // 16], U16, name=f"pos_t{r}") for r in range(2)]
 
-        xw = [keep.tile([P, T], I32, name=f"xw{s}", align_bytes=64) for s in range(2)]
-        xs = share.tile([P, T], U8, name="xs", offset=8 * S - T // 2, align_bytes=64)
-        w1p = [keep.tile([P, 8 * H], U8, name=f"w1_{e}", align_bytes=64) for e in range(2)]
-        w1 = [w1p[e // 2][:, (e % 2) * 4 * H : (e % 2 + 1) * 4 * H] for e in range(E)]
+        zeros = share.tile([P, PAD], F32, name="zeros", offset=XW_AT, align_bytes=64)
+        xw = share.tile([P, 2 * T], I32, name="xw", offset=XW_AT, align_bytes=64)
+        xs = keep.tile([P, 2 * T], U8, name="xs", align_bytes=64)
+        w1p = {lo: keep.tile([P, n * 4 * H], U8, name=f"w1_{lo}", align_bytes=64) for lo, n in W1_LOADS}
+        w1 = [w1p[lo][:, e * 4 * H : (e + 1) * 4 * H] for lo, n in W1_LOADS for e in range(n)]
         w1s = keep.tile([P, E * 2 * H], U8, name="w1s", align_bytes=64)
         w2 = [keep.tile([P, E * K], U8, name=f"w2_{h}", align_bytes=64) for h in range(2)]
         w2s = keep.tile([P, E * K], U8, name="w2s", align_bytes=64)
         y = [keep.tile([P, W], F32, name=f"y{n}") for n in range(NB)]
         ident = keep.tile([P, P], F32, name="ident")
-        warm = keep.tile([P, 8], F32, name="warm")
-        both = [keep.tile([P, size], U8, name=f"both{lo}", align_bytes=64) for lo, size in SCALE_RUNS]
-        moved = [keep.tile([P, size], U8, name=f"moved{lo}", align_bytes=64) for lo, size in SCALE_RUNS]
+        g = keep.tile([P, 2, T], F32, name="g")
 
-        nc.vector.memset(xs[:].bitcast(I32), 0)
+        nc.gpsimd.memset(xs[:].bitcast(I32), 0)
+        nc.vector.memset(zeros[:], 0.0)
+        nc.vector.tensor_copy(y[0][:, S + T : W], zeros[:])
         nc.vector.memset(w1s[:].bitcast(I32), 0)
-        nc.vector.memset(ident[:], 0.0)
-        for tile in moved:
-            nc.vector.memset(tile[:].bitcast(I32), 0)
-        nc.vector.memset(y[0][:, S + T : W], 0.0)
 
-        xw_d = x_words.rearrange("s p t d -> s p (t d)").bitcast(I32)
         nc.sync.dma_start(offs_t[:], offs)
-        nc.scalar.dma_start(xw[0][:], xw_d[0])
-        xs_d = x_scales.bitcast(I32)
-        for q in range(4):
-            nc.sync.dma_start(xs[32 * q : 32 * q + 8, :].bitcast(I32), xs_d[:, 4 * q : 4 * q + 4, :])
-        nc.scalar.activation(warm[:], ident[:, 0:8], SILU)
-        for n in range(1, NB):
+        xs_d = x_scales.bitcast(I32).rearrange("s b t -> b s t")
+        for r in range(4):
+            nc.sync.dma_start(xs[r:P:32, :].bitcast(I32).rearrange("q (s t) -> q s t", s=2), xs_d[r:16:4])
+        nc.sync.dma_start(
+            xw[:].rearrange("p (s t) -> p s t", s=2), x_words.rearrange("s p t d -> p s (t d)").bitcast(I32)
+        )
+        nc.scalar.activation(y[1][:, S + T : W], y[0][:, S + T : W], SILU)
+        for n in range(2, NB):
             nc.scalar.copy(y[n][:, S + T : W], y[0][:, S + T : W])
         w1s_d = w1_scales.bitcast(I32).rearrange("e s b i -> b (e s) i")
         for r in range(4):
@@ -89,60 +94,51 @@ def tile_moe_cpy_mlp_silu_kernel(
         def load_xr(n):
             nc.gpsimd.dma_start(y[n][:, S : S + T], xr[n * P : (n + 1) * P, :])
 
-        def load_w1(h):
+        def load_w1(lo, n):
             nc.gpsimd.dma_start(
-                w1p[h][:].bitcast(I32).rearrange("p (a i) -> p a i", a=4),
-                w1_words[2 * h : 2 * h + 2].bitcast(I32).rearrange("e s p i -> p (e s) i"),
+                w1p[lo][:].bitcast(I32).rearrange("p (a i) -> p a i", a=2 * n),
+                w1_words[lo : lo + n].bitcast(I32).rearrange("e s p i -> p (e s) i"),
             )
 
-        load_w1(0)
-        nc.gpsimd.dma_start(xw[1][:], xw_d[1])
-        make_identity(nc, ident[:], nomemset=True)
+        load_w1(*W1_LOADS[0])
+        make_identity(nc, ident[:])
+        load_w1(*W1_LOADS[1])
         nc.gpsimd.memset(w2s[:].bitcast(I32), 0)
-        load_w1(1)
-
-        for a, (lo, size) in enumerate(SCALE_RUNS):
-            for at in range(0, size, 2 * C):
-                run = min(2 * C, size - at)
-                nc.vector.tensor_copy(
-                    both[a][:, at : at + run], xs[:].indirect(offs_t[:, (lo + at) // 16 : (lo + at + run) // 16])
-                )
-            for q in range(4):
-                nc.scalar.dma_start(
-                    moved[a][32 * q : 32 * q + 4, :].bitcast(I32), both[a][32 * q + 4 : 32 * q + 8, :].bitcast(I32)
-                )
-
+        load_w1(*W1_LOADS[2])
         w2s_d = w2_scales.bitcast(I32).rearrange("e s b n -> b (e s) n")
         for r in range(4):
             nc.sync.dma_start(
                 w2s[r:P:32, :].bitcast(I32).rearrange("q (e n) -> q e n", e=E),
                 w2s_d[r:16:4],
             )
-
-        g = share.tile([P, 2, T], F32, name="g", offset=8 * S, align_bytes=64)
-        nc.gpsimd.dma_start(g[:], gate.rearrange("r p t -> p r t"))
         load_w2(0)
+        nc.gpsimd.dma_start(g[:], gate.rearrange("r p t -> p r t"))
         load_xr(0)
         load_xr(1)
         load_w2(1)
         for n in range(2, NB):
             load_xr(n)
 
-        words = share.tile([P, 2 * S], U32, name="words", offset=0, align_bytes=64)
-        for lo, size in WORD_RUNS:
+        slot_words = {}
+        slot_scales = {}
+
+        def gather_scales(lo, size, offset):
+            tile = share.tile([P, 2 * size], U8, name=f"scales{lo}", offset=offset, align_bytes=64)
             for s in range(2):
+                part = tile[:, s * size : (s + 1) * size]
+                nc.vector.tensor_copy(part, xs[:, s * T : (s + 1) * T].indirect(offs_t[:, lo // 16 : (lo + size) // 16]))
+                for at in range(0, size, P):
+                    slot_scales[lo + at, s] = part[:, at : at + P]
+
+        def gather_words(lo, size, offset):
+            tile = share.tile([P, 2 * size], U32, name=f"words{lo}", offset=offset, align_bytes=64)
+            for s in range(2):
+                part = tile[:, s * size : (s + 1) * size]
                 nc.vector.tensor_copy(
-                    words[:, s * S + lo : s * S + lo + size],
-                    xw[s][:].bitcast(U32).indirect(offs_t[:, lo // 16 : (lo + size) // 16]),
+                    part, xw[:, s * T : (s + 1) * T].bitcast(U32).indirect(offs_t[:, lo // 16 : (lo + size) // 16])
                 )
-
-        def slot_scales(lo, s):
-            a = 0 if lo < C else 1
-            at = lo - SCALE_RUNS[a][0]
-            return (both, moved)[s][a][:, at : at + P]
-
-        codes = [keep.tile([P, C], U32, name=f"codes{e}", align_bytes=64) for e in range(E)]
-        cs = [keep.tile([P, C], U8, name=f"cs{e}", align_bytes=64) for e in range(E)]
+                for at in range(0, size, P):
+                    slot_words[lo + at, s] = part[:, at : at + P]
 
         hb = {}
 
@@ -152,8 +148,8 @@ def tile_moe_cpy_mlp_silu_kernel(
             for s in range(2):
                 nc.tensor.matmul_mx(
                     out=pre[:],
-                    lhsT=words[:, s * S + lo : s * S + lo + P].bitcast(FP8X4),
-                    lhsT_scale=slot_scales(lo, s),
+                    lhsT=slot_words[lo, s].bitcast(FP8X4),
+                    lhsT_scale=slot_scales[lo, s],
                     rhs=w1[e][:, s * 2 * H : (s + 1) * 2 * H].bitcast(FP4X4),
                     rhs_scale=w1s[:, (2 * e + s) * H : (2 * e + s + 1) * H],
                     start=(s == 0),
@@ -166,10 +162,12 @@ def tile_moe_cpy_mlp_silu_kernel(
                 SILU,
             )
 
-        hq = [keep.tile([P, 4 * C], BF16, name=f"hq{e}", align_bytes=64) for e in range(E)]
+        hq = {lo: keep.tile([P, 4 * size], BF16, name=f"hq{lo}", align_bytes=64) for lo, size in GROUPS if lo != 2 * C}
+        hq[2 * C] = share.tile([P, 4 * C], BF16, name="hq_late", offset=XW_AT, align_bytes=64)
 
         def turn(lo, size, copy):
-            e, at = divmod(lo, C)
+            first = max(f for f, n in GROUPS if f <= lo)
+            at = lo - first
             blocks = size // P
             hT = psum.tile([P, blocks, 2, P], F32, name="hT", tag="b")
             for b in range(blocks):
@@ -177,34 +175,36 @@ def tile_moe_cpy_mlp_silu_kernel(
                 for u in range(2):
                     nc.tensor.transpose(hT[:, b, u, :], pairs[:, u * P : (u + 1) * P], ident[:])
             copy(
-                hq[e][:, 4 * at : 4 * (at + size)].bitcast(F32).rearrange("p (b s u) -> p b s u", b=blocks, u=2),
+                hq[first][:, 4 * at : 4 * (at + size)].bitcast(F32).rearrange("p (b s u) -> p b s u", b=blocks, u=2),
                 hT[:].rearrange("p b u s -> p b s u"),
             )
 
+        for first, slots, offset, runs in STAGES:
+            gather_scales(first, slots, offset)
+            for run in runs:
+                gather_words(*run)
+            for lo in range(first, first + slots, P):
+                first_layer(lo)
+            if first == 0:
+                turn(0, C, nc.scalar.copy)
+            if first == 2 * C:
+                turn(C, C, nc.scalar.copy)
+
+        codes = share.tile([P, S], U32, name="codes", offset=XW_AT + 8 * C, align_bytes=64)
+        cs = keep.tile([P, S], U8, name="cs", align_bytes=64)
+
         def quantise(lo, size):
-            e, at = divmod(lo, C)
             nc.vector.quantize_mx(
-                out=codes[e][:, at : at + size].bitcast(FP8X4),
-                scales=cs[e][:, at : at + size],
-                in_=hq[e][:, 4 * at : 4 * (at + size)],
+                out=codes[:, lo : lo + size].bitcast(FP8X4), scales=cs[:, lo : lo + size], in_=hq[lo][:]
             )
 
-        for lo in range(0, 2 * C, P):
-            first_layer(lo)
-        turn(0, C, nc.vector.tensor_copy)
-        quantise(0, C)
-        for lo in range(2 * C, 3 * C, P):
-            first_layer(lo)
-        turn(C, C, nc.vector.tensor_copy)
-        quantise(C, C)
-        for lo in range(3 * C, S, P):
-            first_layer(lo)
         turn(2 * C, C, nc.vector.tensor_copy)
-        quantise(2 * C, C)
+        quantise(*GROUPS[0])
+        quantise(*GROUPS[1])
         turn(3 * C, P, nc.vector.tensor_copy)
-        quantise(3 * C, P)
-        turn(S - P, P, nc.scalar.copy)
-        quantise(S - P, P)
+        turn(S - P, P, nc.vector.tensor_copy)
+        for lo, size in GROUPS[2:]:
+            quantise(lo, size)
 
         def second_layer(acc, n, lo, size):
             h, m = divmod(n, NB // 2)
@@ -216,22 +216,17 @@ def tile_moe_cpy_mlp_silu_kernel(
                     out=acc[:, done : done + run],
                     lhsT=w2[h][:, e * K + m * 2 * P : e * K + (m + 1) * 2 * P].bitcast(FP4X4),
                     lhsT_scale=w2s[:, e * K + n * P : e * K + (n + 1) * P],
-                    rhs=codes[e][:, at : at + run].bitcast(FP8X4),
-                    rhs_scale=cs[e][:, at : at + run],
+                    rhs=codes[:, lo + done : lo + done + run].bitcast(FP8X4),
+                    rhs_scale=cs[:, lo + done : lo + done + run],
                     start=True,
                     stop=True,
                 )
                 done = done + run
 
-        acc = psum.tile([P, 2 * C], F32, name="acc_first", tag="a", bufs=4)
-        second_layer(acc, 0, 0, 2 * C)
-        nc.scalar.copy(y[0][:, 0 : 2 * C], acc[:])
-        acc = psum_y.tile([P, C + P], F32, name="acc", tag="y")
-        second_layer(acc, 0, 2 * C, C + P)
-        nc.vector.tensor_copy(y[0][:, 2 * C : S - P], acc[:])
-        acc = psum_y.tile([P, P], F32, name="acc", tag="y")
-        second_layer(acc, 0, S - P, P)
-        nc.scalar.copy(y[0][:, S - P : S], acc[:])
+        for lo, size in GROUPS:
+            acc = psum.tile([P, size], F32, name="acc_first", tag="a", bufs=4)
+            second_layer(acc, 0, lo, size)
+            nc.scalar.copy(y[0][:, lo : lo + size], acc[:])
 
         def slots_of(n):
             for lo in range(0, S, 2 * C):

@@ -24,14 +24,11 @@ SILU = mybir.ActivationFunctionType.Silu
 
 HALF = T // 2
 KB = 1024
-STAGES = [
-    (0, 512, 6 * KB, [(0, 128, 0), (128, 128, 2 * KB), (256, 256, 4 * KB)]),
-    (512, 256, 0, [(512, 128, KB + KB // 2), (640, 128, 2 * KB + KB // 2)]),
-    (768, 256, 4 * KB, [(768, 128, 5 * KB + KB // 2), (896, 128, 6 * KB + KB // 2)]),
-]
 XW_AT = 8 * KB
+STAGE_BYTES = 3 * KB
+PRE_BANK = [0, 1, 2, 3, 1, 2, 4, 5]
 W1_LOADS = [(0, 1), (1, 1), (2, 2)]
-GROUPS = [(0, 512), (512, 256), (768, 128), (896, 128)]
+GROUPS = [(0, 256), (256, 256), (512, 256), (768, 128), (896, 128)]
 
 
 def tile_moe_cpy_mlp_silu_kernel(
@@ -42,13 +39,14 @@ def tile_moe_cpy_mlp_silu_kernel(
         lists = ctx.enter_context(tc.tile_pool(name="lists", bufs=1))
         keep = ctx.enter_context(tc.tile_pool(name="keep", bufs=1))
         share = ctx.enter_context(tc.tile_pool(name="share", bufs=1))
-        psum = ctx.enter_context(tc.psum_pool(name="psum", bufs=2))
-        psum_y = ctx.enter_context(tc.psum_pool(name="psum_y", bufs=2))
+        psum = ctx.enter_context(tc.psum_pool(name="psum", bufs=1))
+
+        def bank(i, shape):
+            return psum.tile(shape, F32, name=f"bank{i}", tag=f"bank{i}")
 
         offs_t = lists.tile([P, S // 16], U16, name="offs_t")
         pos_t = [lists.tile([P, T // 16], U16, name=f"pos_t{r}") for r in range(2)]
 
-        zeros = share.tile([P, PAD], F32, name="zeros", offset=XW_AT, align_bytes=64)
         xw = share.tile([P, 2 * T], I32, name="xw", offset=XW_AT, align_bytes=64)
         xs = keep.tile([P, 2 * T], U8, name="xs", align_bytes=64)
         w1p = {lo: keep.tile([P, n * 4 * H], U8, name=f"w1_{lo}", align_bytes=64) for lo, n in W1_LOADS}
@@ -61,59 +59,50 @@ def tile_moe_cpy_mlp_silu_kernel(
         g = keep.tile([P, 2, T], F32, name="g")
 
         nc.gpsimd.memset(xs[:].bitcast(I32), 0)
-        nc.vector.memset(zeros[:], 0.0)
-        nc.vector.tensor_copy(y[0][:, S + T : W], zeros[:])
         nc.vector.memset(w1s[:].bitcast(I32), 0)
-
-        nc.sync.dma_start(offs_t[:], offs)
-        xs_d = x_scales.bitcast(I32).rearrange("s b t -> b s t")
-        for r in range(4):
-            nc.sync.dma_start(xs[r:P:32, :].bitcast(I32).rearrange("q (s t) -> q s t", s=2), xs_d[r:16:4])
-        nc.sync.dma_start(
-            xw[:].rearrange("p (s t) -> p s t", s=2), x_words.rearrange("s p t d -> p s (t d)").bitcast(I32)
-        )
+        nc.vector.memset(y[0][:, S + T : W], 0.0)
+        make_identity(nc, ident[:])
+        nc.gpsimd.memset(w2s[:].bitcast(I32), 0)
         nc.scalar.activation(y[1][:, S + T : W], y[0][:, S + T : W], SILU)
         for n in range(2, NB):
             nc.scalar.copy(y[n][:, S + T : W], y[0][:, S + T : W])
-        w1s_d = w1_scales.bitcast(I32).rearrange("e s b i -> b (e s) i")
-        for r in range(4):
-            nc.sync.dma_start(
-                w1s[r:P:32, :].bitcast(I32).rearrange("q (a i) -> q a i", a=2 * E),
-                w1s_d[r:16:4],
-            )
-        nc.sync.dma_start(pos_t[0][:], pos1)
-        nc.sync.dma_start(pos_t[1][:], pos2)
-        w2_d = w2_words.bitcast(I32).rearrange("e s p n -> p (e s) n")
 
-        def load_w2(h):
-            nc.gpsimd.dma_start(
-                w2[h][:].bitcast(I32).rearrange("p (e n) -> p e n", e=E),
-                w2_d[:, :, h * (K // 4) : (h + 1) * (K // 4)],
-            )
-
-        def load_xr(n):
-            nc.gpsimd.dma_start(y[n][:, S : S + T], xr[n * P : (n + 1) * P, :])
+        def load_scale_rows(tile, rows, queues):
+            for r in range(4):
+                queues[r % len(queues)].dma_start(
+                    tile[r:P:32, :].bitcast(I32).rearrange("q (a i) -> q a i", a=rows.shape[1]), rows[r:16:4]
+                )
 
         def load_w1(lo, n):
-            nc.gpsimd.dma_start(
+            nc.sync.dma_start(
                 w1p[lo][:].bitcast(I32).rearrange("p (a i) -> p a i", a=2 * n),
                 w1_words[lo : lo + n].bitcast(I32).rearrange("e s p i -> p (e s) i"),
             )
 
-        load_w1(*W1_LOADS[0])
-        make_identity(nc, ident[:])
-        load_w1(*W1_LOADS[1])
-        nc.gpsimd.memset(w2s[:].bitcast(I32), 0)
-        load_w1(*W1_LOADS[2])
-        w2s_d = w2_scales.bitcast(I32).rearrange("e s b n -> b (e s) n")
-        for r in range(4):
+        def load_w2(h):
             nc.sync.dma_start(
-                w2s[r:P:32, :].bitcast(I32).rearrange("q (e n) -> q e n", e=E),
-                w2s_d[r:16:4],
+                w2[h][:].bitcast(I32).rearrange("p (e n) -> p e n", e=E),
+                w2_words.bitcast(I32).rearrange("e s p n -> p (e s) n")[:, :, h * (K // 4) : (h + 1) * (K // 4)],
             )
+
+        def load_xr(n):
+            nc.sync.dma_start(y[n][:, S : S + T], xr[n * P : (n + 1) * P, :])
+
+        nc.sync.dma_start(offs_t[:], offs)
+        load_scale_rows(xs, x_scales.bitcast(I32).rearrange("s b t -> b s t"), (nc.sync, nc.scalar))
+        nc.sync.dma_start(
+            xw[:].rearrange("p (s t) -> p s t", s=2), x_words.rearrange("s p t d -> p s (t d)").bitcast(I32)
+        )
+        load_w1(*W1_LOADS[0])
+        load_scale_rows(w1s, w1_scales.bitcast(I32).rearrange("e s b i -> b (e s) i"), (nc.sync,))
+        load_w1(*W1_LOADS[1])
+        load_w1(*W1_LOADS[2])
+        nc.sync.dma_start(pos_t[0][:], pos1)
+        nc.sync.dma_start(pos_t[1][:], pos2)
+        load_scale_rows(w2s, w2_scales.bitcast(I32).rearrange("e s b n -> b (e s) n"), (nc.sync,))
         load_w2(0)
-        nc.gpsimd.dma_start(g[:], gate.rearrange("r p t -> p r t"))
         load_xr(0)
+        nc.sync.dma_start(g[:], gate.rearrange("r p t -> p r t"))
         load_xr(1)
         load_w2(1)
         for n in range(2, NB):
@@ -122,39 +111,38 @@ def tile_moe_cpy_mlp_silu_kernel(
         slot_words = {}
         slot_scales = {}
 
-        def gather_scales(lo, size, offset):
-            tile = share.tile([P, 2 * size], U8, name=f"scales{lo}", offset=offset, align_bytes=64)
-            for s in range(2):
-                part = tile[:, s * size : (s + 1) * size]
-                nc.vector.tensor_copy(part, xs[:, s * T : (s + 1) * T].indirect(offs_t[:, lo // 16 : (lo + size) // 16]))
-                for at in range(0, size, P):
-                    slot_scales[lo + at, s] = part[:, at : at + P]
+        def gather_scales(tile, lo, size, s):
+            nc.vector.tensor_copy(tile, xs[:, s * T : (s + 1) * T].indirect(offs_t[:, lo // 16 : (lo + size) // 16]))
+            for at in range(0, size, P):
+                slot_scales[lo + at, s] = tile[:, at : at + P]
 
-        def gather_words(lo, size, offset):
-            tile = share.tile([P, 2 * size], U32, name=f"words{lo}", offset=offset, align_bytes=64)
-            for s in range(2):
-                part = tile[:, s * size : (s + 1) * size]
-                nc.vector.tensor_copy(
-                    part, xw[:, s * T : (s + 1) * T].bitcast(U32).indirect(offs_t[:, lo // 16 : (lo + size) // 16])
-                )
-                for at in range(0, size, P):
-                    slot_words[lo + at, s] = part[:, at : at + P]
+        def gather_words(tile, lo, size, s):
+            nc.vector.tensor_copy(
+                tile, xw[:, s * T : (s + 1) * T].bitcast(U32).indirect(offs_t[:, lo // 16 : (lo + size) // 16])
+            )
+            for at in range(0, size, P):
+                slot_words[lo + at, s] = tile[:, at : at + P]
 
         hb = {}
 
-        def first_layer(lo):
+        pres = {}
+
+        def first_pass(lo, s):
             e = lo // C
-            pre = psum.tile([P, H], F32, name="pre", tag="a", bufs=4)
-            for s in range(2):
-                nc.tensor.matmul_mx(
-                    out=pre[:],
-                    lhsT=slot_words[lo, s].bitcast(FP8X4),
-                    lhsT_scale=slot_scales[lo, s],
-                    rhs=w1[e][:, s * 2 * H : (s + 1) * 2 * H].bitcast(FP4X4),
-                    rhs_scale=w1s[:, (2 * e + s) * H : (2 * e + s + 1) * H],
-                    start=(s == 0),
-                    stop=(s == 1),
-                )
+            if s == 0:
+                pres[lo] = bank(PRE_BANK[lo // P], [P, H])
+            nc.tensor.matmul_mx(
+                out=pres[lo][:],
+                lhsT=slot_words[lo, s].bitcast(FP8X4),
+                lhsT_scale=slot_scales[lo, s],
+                rhs=w1[e][:, s * 2 * H : (s + 1) * 2 * H].bitcast(FP4X4),
+                rhs_scale=w1s[:, (2 * e + s) * H : (2 * e + s + 1) * H],
+                start=(s == 0),
+                stop=(s == 1),
+            )
+
+        def activate(lo):
+            pre = pres[lo]
             hb[lo] = keep.tile([P, H], BF16, name=f"hb{lo}")
             nc.scalar.activation(
                 hb[lo][:].rearrange("s (u p d) -> s u p d", u=2, d=2),
@@ -162,14 +150,14 @@ def tile_moe_cpy_mlp_silu_kernel(
                 SILU,
             )
 
-        hq = {lo: keep.tile([P, 4 * size], BF16, name=f"hq{lo}", align_bytes=64) for lo, size in GROUPS if lo != 2 * C}
-        hq[2 * C] = share.tile([P, 4 * C], BF16, name="hq_late", offset=XW_AT, align_bytes=64)
+        hq = {lo: keep.tile([P, 4 * size], BF16, name=f"hq{lo}", align_bytes=64) for lo, size in GROUPS if lo != C}
+        hq[C] = share.tile([P, 4 * C], BF16, name="hq_late", offset=XW_AT, align_bytes=64)
 
-        def turn(lo, size, copy):
+        def turn(lo, size, copy, where):
             first = max(f for f, n in GROUPS if f <= lo)
             at = lo - first
             blocks = size // P
-            hT = psum.tile([P, blocks, 2, P], F32, name="hT", tag="b")
+            hT = bank(where, [P, blocks, 2, P])
             for b in range(blocks):
                 pairs = hb[lo + b * P][:].bitcast(F32)
                 for u in range(2):
@@ -179,18 +167,46 @@ def tile_moe_cpy_mlp_silu_kernel(
                 hT[:].rearrange("p b u s -> p b s u"),
             )
 
-        for first, slots, offset, runs in STAGES:
-            gather_scales(first, slots, offset)
-            for run in runs:
-                gather_words(*run)
-            for lo in range(first, first + slots, P):
-                first_layer(lo)
-            if first == 0:
-                turn(0, C, nc.scalar.copy)
-            if first == 2 * C:
-                turn(C, C, nc.scalar.copy)
+        scales = keep.tile([P, S], U8, name="scales", align_bytes=64)
+        for s in range(2):
+            gather_scales(scales[:, s * 2 * C : (s + 1) * 2 * C], 0, 2 * C, s)
+        runs = [
+            (0, P, share.tile([P, STAGE_BYTES // 4], U32, name="words_a", offset=0, align_bytes=64)),
+            (P, P, keep.tile([P, 2 * P], U32, name="words_b", align_bytes=64)),
+            (C, C, share.tile([P, STAGE_BYTES // 4], U32, name="words_c", offset=STAGE_BYTES, align_bytes=64)),
+        ]
+        for lo, size, tile in runs:
+            for s in range(2):
+                gather_words(tile[:, s * size : (s + 1) * size], lo, size, s)
+        for lo in range(0, 2 * C, P):
+            for s in range(2):
+                first_pass(lo, s)
+            activate(lo)
+        turn(0, P, nc.scalar.copy, 4)
+        turn(P, P, nc.scalar.copy, 5)
+        turn(C, C, nc.vector.tensor_copy, 0)
+        for e in range(2, E):
+            at = (e - 2) * STAGE_BYTES
+            scales = share.tile([P, 2 * C], U8, name=f"scales{e}", offset=at, align_bytes=64)
+            words = share.tile([P, 2 * C], U32, name=f"words{e}", offset=at + 2 * C, align_bytes=64)
+            if e == 2:
+                for s in range(2):
+                    gather_scales(scales[:, s * C : (s + 1) * C], e * C, C, s)
+                    gather_words(words[:, s * C : (s + 1) * C], e * C, C, s)
+                    for b in range(0, C, P):
+                        first_pass(e * C + b, s)
+                        if s == 1:
+                            activate(e * C + b)
+            else:
+                for s in range(2):
+                    gather_scales(scales[:, s * C : (s + 1) * C], e * C, C, s)
+                for b in range(0, C, P):
+                    for s in range(2):
+                        gather_words(words[:, s * C + b : s * C + b + P], e * C + b, P, s)
+                        first_pass(e * C + b, s)
+                    activate(e * C + b)
 
-        codes = share.tile([P, S], U32, name="codes", offset=XW_AT + 8 * C, align_bytes=64)
+        codes = share.tile([P, S], U32, name="codes", offset=XW_AT + 16 * C, align_bytes=64)
         cs = keep.tile([P, S], U8, name="cs", align_bytes=64)
 
         def quantise(lo, size):
@@ -198,13 +214,14 @@ def tile_moe_cpy_mlp_silu_kernel(
                 out=codes[:, lo : lo + size].bitcast(FP8X4), scales=cs[:, lo : lo + size], in_=hq[lo][:]
             )
 
-        turn(2 * C, C, nc.vector.tensor_copy)
         quantise(*GROUPS[0])
         quantise(*GROUPS[1])
-        turn(3 * C, P, nc.vector.tensor_copy)
-        turn(S - P, P, nc.vector.tensor_copy)
-        for lo, size in GROUPS[2:]:
-            quantise(lo, size)
+        turn(2 * C, C, nc.vector.tensor_copy, 3)
+        turn(3 * C, P, nc.scalar.copy, 6)
+        turn(S - P, P, nc.scalar.copy, 7)
+        quantise(*GROUPS[3])
+        quantise(*GROUPS[2])
+        quantise(*GROUPS[4])
 
         def second_layer(acc, n, lo, size):
             h, m = divmod(n, NB // 2)
@@ -223,14 +240,19 @@ def tile_moe_cpy_mlp_silu_kernel(
                 )
                 done = done + run
 
-        for lo, size in GROUPS:
-            acc = psum.tile([P, size], F32, name="acc_first", tag="a", bufs=4)
+        for lo, size, where, copy in (
+            (0, 2 * C, 0, nc.scalar.copy),
+            (3 * C, P, 4, nc.vector.tensor_copy),
+            (2 * C, C, 2, nc.scalar.copy),
+            (S - P, P, 5, nc.vector.tensor_copy),
+        ):
+            acc = bank(where, [P, size])
             second_layer(acc, 0, lo, size)
-            nc.scalar.copy(y[0][:, lo : lo + size], acc[:])
+            copy(y[0][:, lo : lo + size], acc[:])
 
         def slots_of(n):
             for lo in range(0, S, 2 * C):
-                acc = psum_y.tile([P, 2 * C], F32, name="acc", tag="y")
+                acc = bank(4 + 2 * (n % 2) + lo // (2 * C), [P, 2 * C])
                 second_layer(acc, n, lo, 2 * C)
                 nc.scalar.copy(y[n][:, lo : lo + 2 * C], acc[:])
 
@@ -245,7 +267,7 @@ def tile_moe_cpy_mlp_silu_kernel(
             a = [weighted(n, r, 0, T) for r in range(2)]
             turned = []
             for at in range(0, T, HALF):
-                sumT = psum.tile([P, HALF], F32, name="sumT", tag="a", bufs=4)
+                sumT = bank(2 * (n % 2) + at // HALF, [P, HALF])
                 for j in range(0, HALF, P):
                     for r in range(2):
                         nc.tensor.matmul(
@@ -263,7 +285,7 @@ def tile_moe_cpy_mlp_silu_kernel(
         def turn_back(n, turned):
             res = keep.tile([P, T], F32, name="res", bufs=4)
             for i, t in enumerate(turned):
-                back = psum.tile([P, HALF], F32, name="back", tag="b")
+                back = bank(2 * ((n + 1) % 2) + i, [P, HALF])
                 for j in range(0, HALF, P):
                     nc.tensor.transpose(back[:, j : j + P], t[:, j : j + P], ident[:])
                 nc.scalar.copy(res[:, i * HALF : (i + 1) * HALF], back[:])
@@ -283,8 +305,9 @@ def tile_moe_cpy_mlp_silu_kernel(
                 slots_of(5 + 2 * n)
 
         n = NB - 1
-        a = [weighted(n, r, 0, T) for r in range(2)]
+        first = weighted(n, 0, 0, T)
+        second = [weighted(n, 1, at, HALF) for at in range(0, T, HALF)]
         for at in range(0, T, HALF):
             res = keep.tile([P, HALF], F32, name="res_last", tag=f"last{at}")
-            nc.vector.tensor_tensor(res[:], a[0][:, at : at + HALF], a[1][:, at : at + HALF], ADD)
+            nc.vector.tensor_tensor(res[:], first[:, at : at + HALF], second[at // HALF][:], ADD)
             nc.sync.dma_start(out[n * P : (n + 1) * P, at : at + HALF], res[:])

@@ -23,12 +23,15 @@ ADD = mybir.AluOpType.add
 SILU = mybir.ActivationFunctionType.Silu
 
 HALF = T // 2
-KB = 1024
-XW_AT = 8 * KB
-STAGE_BYTES = 3 * KB
+AHEAD = 4
+RING = 4
+
+EXPERT_BYTES = 3 * 1024
+TOKENS_AT = 8 * 1024
+
 PRE_BANK = [0, 1, 2, 3, 1, 2, 4, 5]
 W1_LOADS = [(0, 1), (1, 1), (2, 2)]
-GROUPS = [(0, 256), (256, 256), (512, 256), (768, 128), (896, 128)]
+GROUPS = [(0, C), (C, C), (2 * C, C), (3 * C, P), (S - P, P)]
 
 
 def tile_moe_cpy_mlp_silu_kernel(
@@ -47,10 +50,10 @@ def tile_moe_cpy_mlp_silu_kernel(
         offs_t = lists.tile([P, S // 16], U16, name="offs_t")
         pos_t = [lists.tile([P, T // 16], U16, name=f"pos_t{r}") for r in range(2)]
 
-        xw = share.tile([P, 2 * T], I32, name="xw", offset=XW_AT, align_bytes=64)
+        xw = share.tile([P, 2 * T], I32, name="xw", offset=TOKENS_AT, align_bytes=64)
         xs = keep.tile([P, 2 * T], U8, name="xs", align_bytes=64)
-        w1p = {lo: keep.tile([P, n * 4 * H], U8, name=f"w1_{lo}", align_bytes=64) for lo, n in W1_LOADS}
-        w1 = [w1p[lo][:, e * 4 * H : (e + 1) * 4 * H] for lo, n in W1_LOADS for e in range(n)]
+        w1_tiles = {e0: keep.tile([P, n * 4 * H], U8, name=f"w1_{e0}", align_bytes=64) for e0, n in W1_LOADS}
+        w1 = [w1_tiles[e0][:, j * 4 * H : (j + 1) * 4 * H] for e0, n in W1_LOADS for j in range(n)]
         w1s = keep.tile([P, E * 2 * H], U8, name="w1s", align_bytes=64)
         w2 = [keep.tile([P, E * K], U8, name=f"w2_{h}", align_bytes=64) for h in range(2)]
         w2s = keep.tile([P, E * K], U8, name="w2s", align_bytes=64)
@@ -73,10 +76,10 @@ def tile_moe_cpy_mlp_silu_kernel(
                     tile[r:P:32, :].bitcast(I32).rearrange("q (a i) -> q a i", a=rows.shape[1]), rows[r:16:4]
                 )
 
-        def load_w1(lo, n):
+        def load_w1(e0, n):
             nc.sync.dma_start(
-                w1p[lo][:].bitcast(I32).rearrange("p (a i) -> p a i", a=2 * n),
-                w1_words[lo : lo + n].bitcast(I32).rearrange("e s p i -> p (e s) i"),
+                w1_tiles[e0][:].bitcast(I32).rearrange("p (a i) -> p a i", a=2 * n),
+                w1_words[e0 : e0 + n].bitcast(I32).rearrange("e s p i -> p (e s) i"),
             )
 
         def load_w2(h):
@@ -111,28 +114,27 @@ def tile_moe_cpy_mlp_silu_kernel(
         slot_words = {}
         slot_scales = {}
 
-        def gather_scales(tile, lo, size, s):
-            nc.vector.tensor_copy(tile, xs[:, s * T : (s + 1) * T].indirect(offs_t[:, lo // 16 : (lo + size) // 16]))
+        def gather_scales(dst, lo, size, s):
+            nc.vector.tensor_copy(dst, xs[:, s * T : (s + 1) * T].indirect(offs_t[:, lo // 16 : (lo + size) // 16]))
             for at in range(0, size, P):
-                slot_scales[lo + at, s] = tile[:, at : at + P]
+                slot_scales[lo + at, s] = dst[:, at : at + P]
 
-        def gather_words(tile, lo, size, s):
+        def gather_words(dst, lo, size, s):
             nc.vector.tensor_copy(
-                tile, xw[:, s * T : (s + 1) * T].bitcast(U32).indirect(offs_t[:, lo // 16 : (lo + size) // 16])
+                dst, xw[:, s * T : (s + 1) * T].bitcast(U32).indirect(offs_t[:, lo // 16 : (lo + size) // 16])
             )
             for at in range(0, size, P):
-                slot_words[lo + at, s] = tile[:, at : at + P]
+                slot_words[lo + at, s] = dst[:, at : at + P]
 
+        pre = {}
         hb = {}
-
-        pres = {}
 
         def first_pass(lo, s):
             e = lo // C
             if s == 0:
-                pres[lo] = bank(PRE_BANK[lo // P], [P, H])
+                pre[lo] = bank(PRE_BANK[lo // P], [P, H])
             nc.tensor.matmul_mx(
-                out=pres[lo][:],
+                out=pre[lo][:],
                 lhsT=slot_words[lo, s].bitcast(FP8X4),
                 lhsT_scale=slot_scales[lo, s],
                 rhs=w1[e][:, s * 2 * H : (s + 1) * 2 * H].bitcast(FP4X4),
@@ -142,20 +144,19 @@ def tile_moe_cpy_mlp_silu_kernel(
             )
 
         def activate(lo):
-            pre = pres[lo]
             hb[lo] = keep.tile([P, H], BF16, name=f"hb{lo}")
             nc.scalar.activation(
                 hb[lo][:].rearrange("s (u p d) -> s u p d", u=2, d=2),
-                pre[:].rearrange("s (p u d) -> s u p d", u=2, d=2),
+                pre[lo][:].rearrange("s (p u d) -> s u p d", u=2, d=2),
                 SILU,
             )
 
         hq = {lo: keep.tile([P, 4 * size], BF16, name=f"hq{lo}", align_bytes=64) for lo, size in GROUPS if lo != C}
-        hq[C] = share.tile([P, 4 * C], BF16, name="hq_late", offset=XW_AT, align_bytes=64)
+        hq[C] = share.tile([P, 4 * C], BF16, name="hq_late", offset=TOKENS_AT, align_bytes=64)
 
         def turn(lo, size, copy, where):
-            first = max(f for f, n in GROUPS if f <= lo)
-            at = lo - first
+            group = max(f for f, n in GROUPS if f <= lo)
+            at = lo - group
             blocks = size // P
             hT = bank(where, [P, blocks, 2, P])
             for b in range(blocks):
@@ -163,7 +164,7 @@ def tile_moe_cpy_mlp_silu_kernel(
                 for u in range(2):
                     nc.tensor.transpose(hT[:, b, u, :], pairs[:, u * P : (u + 1) * P], ident[:])
             copy(
-                hq[first][:, 4 * at : 4 * (at + size)].bitcast(F32).rearrange("p (b s u) -> p b s u", b=blocks, u=2),
+                hq[group][:, 4 * at : 4 * (at + size)].bitcast(F32).rearrange("p (b s u) -> p b s u", b=blocks, u=2),
                 hT[:].rearrange("p b u s -> p b s u"),
             )
 
@@ -171,9 +172,9 @@ def tile_moe_cpy_mlp_silu_kernel(
         for s in range(2):
             gather_scales(scales[:, s * 2 * C : (s + 1) * 2 * C], 0, 2 * C, s)
         runs = [
-            (0, P, share.tile([P, STAGE_BYTES // 4], U32, name="words_a", offset=0, align_bytes=64)),
+            (0, P, share.tile([P, EXPERT_BYTES // 4], U32, name="words_a", offset=0, align_bytes=64)),
             (P, P, keep.tile([P, 2 * P], U32, name="words_b", align_bytes=64)),
-            (C, C, share.tile([P, STAGE_BYTES // 4], U32, name="words_c", offset=STAGE_BYTES, align_bytes=64)),
+            (C, C, share.tile([P, EXPERT_BYTES // 4], U32, name="words_c", offset=EXPERT_BYTES, align_bytes=64)),
         ]
         for lo, size, tile in runs:
             for s in range(2):
@@ -185,28 +186,32 @@ def tile_moe_cpy_mlp_silu_kernel(
         turn(0, P, nc.scalar.copy, 4)
         turn(P, P, nc.scalar.copy, 5)
         turn(C, C, nc.vector.tensor_copy, 0)
-        for e in range(2, E):
-            at = (e - 2) * STAGE_BYTES
-            scales = share.tile([P, 2 * C], U8, name=f"scales{e}", offset=at, align_bytes=64)
-            words = share.tile([P, 2 * C], U32, name=f"words{e}", offset=at + 2 * C, align_bytes=64)
-            if e == 2:
-                for s in range(2):
-                    gather_scales(scales[:, s * C : (s + 1) * C], e * C, C, s)
-                    gather_words(words[:, s * C : (s + 1) * C], e * C, C, s)
-                    for b in range(0, C, P):
-                        first_pass(e * C + b, s)
-                        if s == 1:
-                            activate(e * C + b)
-            else:
-                for s in range(2):
-                    gather_scales(scales[:, s * C : (s + 1) * C], e * C, C, s)
-                for b in range(0, C, P):
-                    for s in range(2):
-                        gather_words(words[:, s * C + b : s * C + b + P], e * C + b, P, s)
-                        first_pass(e * C + b, s)
-                    activate(e * C + b)
 
-        codes = share.tile([P, S], U32, name="codes", offset=XW_AT + 16 * C, align_bytes=64)
+        def room(e):
+            at = (e - 2) * EXPERT_BYTES
+            return (
+                share.tile([P, 2 * C], U8, name=f"scales{e}", offset=at, align_bytes=64),
+                share.tile([P, 2 * C], U32, name=f"words{e}", offset=at + 2 * C, align_bytes=64),
+            )
+
+        scales, words = room(2)
+        for s in range(2):
+            gather_scales(scales[:, s * C : (s + 1) * C], 2 * C, C, s)
+            gather_words(words[:, s * C : (s + 1) * C], 2 * C, C, s)
+            for lo in range(2 * C, 3 * C, P):
+                first_pass(lo, s)
+                if s == 1:
+                    activate(lo)
+        scales, words = room(3)
+        for s in range(2):
+            gather_scales(scales[:, s * C : (s + 1) * C], 3 * C, C, s)
+        for b in range(0, C, P):
+            for s in range(2):
+                gather_words(words[:, s * C + b : s * C + b + P], 3 * C + b, P, s)
+                first_pass(3 * C + b, s)
+            activate(3 * C + b)
+
+        codes = share.tile([P, S], U32, name="codes", offset=TOKENS_AT + 4 * S, align_bytes=64)
         cs = keep.tile([P, S], U8, name="cs", align_bytes=64)
 
         def quantise(lo, size):
@@ -252,7 +257,7 @@ def tile_moe_cpy_mlp_silu_kernel(
 
         def slots_of(n):
             for lo in range(0, S, 2 * C):
-                acc = bank(4 + 2 * (n % 2) + lo // (2 * C), [P, 2 * C])
+                acc = bank(6 + lo // (2 * C), [P, 2 * C])
                 second_layer(acc, n, lo, 2 * C)
                 nc.scalar.copy(y[n][:, lo : lo + 2 * C], acc[:])
 
@@ -263,51 +268,59 @@ def tile_moe_cpy_mlp_silu_kernel(
             )
             return a
 
+        LAST_TURNED = NB - 2
+
         def turn_and_add(n):
-            a = [weighted(n, r, 0, T) for r in range(2)]
+            if n < LAST_TURNED:
+                whole = [weighted(n, r, 0, T) for r in range(2)]
             turned = []
             for at in range(0, T, HALF):
+                if n < LAST_TURNED:
+                    a = [whole[r][:, at : at + HALF] for r in range(2)]
+                else:
+                    a = [weighted(n, r, at, HALF)[:] for r in range(2)]
                 sumT = bank(2 * (n % 2) + at // HALF, [P, HALF])
                 for j in range(0, HALF, P):
                     for r in range(2):
                         nc.tensor.matmul(
-                            sumT[:, j : j + P], a[r][:, at + j : at + j + P], ident[:],
+                            sumT[:, j : j + P], a[r][:, j : j + P], ident[:],
                             start=(r == 0), stop=(r == 1), is_transpose=True,
                         )
-                if n == NB - 2:
+                if n == LAST_TURNED:
                     t = keep.tile([P, HALF], F32, name="turned", tag=f"last{at}")
                 else:
-                    t = keep.tile([P, HALF], F32, name="turned", bufs=4)
+                    t = keep.tile([P, HALF], F32, name="turned", bufs=RING)
                 nc.scalar.copy(t[:], sumT[:])
                 turned.append(t)
             return turned
 
         def turn_back(n, turned):
-            res = keep.tile([P, T], F32, name="res", bufs=4)
+            res = keep.tile([P, T], F32, name="res", bufs=RING)
             for i, t in enumerate(turned):
-                back = bank(2 * ((n + 1) % 2) + i, [P, HALF])
+                back = bank(4 + i, [P, HALF])
                 for j in range(0, HALF, P):
                     nc.tensor.transpose(back[:, j : j + P], t[:, j : j + P], ident[:])
-                nc.scalar.copy(res[:, i * HALF : (i + 1) * HALF], back[:])
-                if n == NB - 2:
-                    nc.sync.dma_start(out[n * P : (n + 1) * P, i * HALF : (i + 1) * HALF], res[:, i * HALF : (i + 1) * HALF])
-            if n != NB - 2:
+                cols = slice(i * HALF, (i + 1) * HALF)
+                nc.scalar.copy(res[:, cols], back[:])
+                if n == LAST_TURNED:
+                    nc.sync.dma_start(out[n * P : (n + 1) * P, cols], res[:, cols])
+            if n != LAST_TURNED:
                 nc.sync.dma_start(out[n * P : (n + 1) * P, :], res[:])
 
-        for n in range(1, 4):
+        for n in range(1, AHEAD):
             slots_of(n)
-        for n in range(NB - 1):
+        for n in range(LAST_TURNED + 1):
             turned = turn_and_add(n)
-            if 4 + 2 * n < NB:
-                slots_of(4 + 2 * n)
+            if AHEAD + 2 * n < NB:
+                slots_of(AHEAD + 2 * n)
             turn_back(n, turned)
-            if 5 + 2 * n < NB:
-                slots_of(5 + 2 * n)
+            if AHEAD + 2 * n + 1 < NB:
+                slots_of(AHEAD + 2 * n + 1)
 
         n = NB - 1
         first = weighted(n, 0, 0, T)
         second = [weighted(n, 1, at, HALF) for at in range(0, T, HALF)]
         for at in range(0, T, HALF):
-            res = keep.tile([P, HALF], F32, name="res_last", tag=f"last{at}")
-            nc.vector.tensor_tensor(res[:], first[:, at : at + HALF], second[at // HALF][:], ADD)
-            nc.sync.dma_start(out[n * P : (n + 1) * P, at : at + HALF], res[:])
+            res_last = keep.tile([P, HALF], F32, name="res_last", tag=f"last{at}")
+            nc.vector.tensor_tensor(res_last[:], first[:, at : at + HALF], second[at // HALF][:], ADD)
+            nc.sync.dma_start(out[n * P : (n + 1) * P, at : at + HALF], res_last[:])

@@ -26,12 +26,11 @@ HALF = T // 2
 AHEAD = 4
 RING = 4
 
-EXPERT_BYTES = 3 * 1024
-TOKENS_AT = 8 * 1024
-
-PRE_BANK = [0, 1, 2, 3, 1, 2, 4, 5]
+SHIFT = 16
 W1_LOADS = [(0, 1), (1, 1), (2, 2)]
 GROUPS = [(0, C), (C, C), (2 * C, C), (3 * C, P), (S - P, P)]
+WORD_RUNS = [(0, P, 0), (0, P, 1), (P, P, 0), (P, P, 1), (C, C, 0), (C, C, 1), (2 * C, C, 0), (2 * C, C, 1),
+             (3 * C, C, 0), (3 * C, P, 1), (S - P, P, 1)]
 
 
 def tile_moe_cpy_mlp_silu_kernel(
@@ -41,7 +40,6 @@ def tile_moe_cpy_mlp_silu_kernel(
     with ExitStack() as ctx:
         lists = ctx.enter_context(tc.tile_pool(name="lists", bufs=1))
         keep = ctx.enter_context(tc.tile_pool(name="keep", bufs=1))
-        share = ctx.enter_context(tc.tile_pool(name="share", bufs=1))
         psum = ctx.enter_context(tc.psum_pool(name="psum", bufs=1))
 
         def bank(i, shape):
@@ -50,8 +48,10 @@ def tile_moe_cpy_mlp_silu_kernel(
         offs_t = lists.tile([P, S // 16], U16, name="offs_t")
         pos_t = [lists.tile([P, T // 16], U16, name=f"pos_t{r}") for r in range(2)]
 
-        xw = share.tile([P, 2 * T], I32, name="xw", offset=TOKENS_AT, align_bytes=64)
-        xs = keep.tile([P, 2 * T], U8, name="xs", align_bytes=64)
+        xw = keep.tile([P, 2 * T], I32, name="xw", align_bytes=64)
+        xs = keep.tile([P, T], U8, name="xs", align_bytes=64)
+        scales = keep.tile([P, S], U8, name="scales", align_bytes=64)
+        moved = keep.tile([P, S], U8, name="moved", align_bytes=64)
         w1_tiles = {e0: keep.tile([P, n * 4 * H], U8, name=f"w1_{e0}", align_bytes=64) for e0, n in W1_LOADS}
         w1 = [w1_tiles[e0][:, j * 4 * H : (j + 1) * 4 * H] for e0, n in W1_LOADS for j in range(n)]
         w1s = keep.tile([P, E * 2 * H], U8, name="w1s", align_bytes=64)
@@ -63,6 +63,7 @@ def tile_moe_cpy_mlp_silu_kernel(
 
         nc.gpsimd.memset(xs[:].bitcast(I32), 0)
         nc.vector.memset(w1s[:].bitcast(I32), 0)
+        nc.vector.memset(moved[96:P, :].bitcast(I32), 0)
         nc.vector.memset(y[0][:, S + T : W], 0.0)
         make_identity(nc, ident[:])
         nc.gpsimd.memset(w2s[:].bitcast(I32), 0)
@@ -92,14 +93,19 @@ def tile_moe_cpy_mlp_silu_kernel(
             nc.sync.dma_start(y[n][:, S : S + T], xr[n * P : (n + 1) * P, :])
 
         nc.sync.dma_start(offs_t[:], offs)
-        load_scale_rows(xs, x_scales.bitcast(I32).rearrange("s b t -> b s t"), (nc.sync, nc.scalar))
+        xs_rows = x_scales.bitcast(I32).rearrange("s b t -> b s t")
+        for r in range(4):
+            (nc.sync, nc.scalar)[r % 2].dma_start(xs[r:P:SHIFT, :].bitcast(I32), xs_rows[r:16:4])
         nc.sync.dma_start(
             xw[:].rearrange("p (s t) -> p s t", s=2), x_words.rearrange("s p t d -> p s (t d)").bitcast(I32)
         )
-        load_w1(*W1_LOADS[0])
         load_scale_rows(w1s, w1_scales.bitcast(I32).rearrange("e s b i -> b (e s) i"), (nc.sync,))
+        load_w1(*W1_LOADS[0])
         load_w1(*W1_LOADS[1])
         load_w1(*W1_LOADS[2])
+        for lo, hi, queue in ((0, C, nc.scalar), (C, 2 * C, nc.scalar), (2 * C, S, nc.sync)):
+            nc.vector.tensor_copy(scales[:, lo:hi], xs[:].indirect(offs_t[:, lo // 16 : hi // 16]))
+            queue.dma_start(moved[0 : P - SHIFT, lo:hi].bitcast(I32), scales[SHIFT:P, lo:hi].bitcast(I32))
         nc.sync.dma_start(pos_t[0][:], pos1)
         nc.sync.dma_start(pos_t[1][:], pos2)
         load_scale_rows(w2s, w2_scales.bitcast(I32).rearrange("e s b n -> b (e s) n"), (nc.sync,))
@@ -112,51 +118,40 @@ def tile_moe_cpy_mlp_silu_kernel(
             load_xr(n)
 
         slot_words = {}
-        slot_scales = {}
-
-        def gather_scales(dst, lo, size, s):
-            nc.vector.tensor_copy(dst, xs[:, s * T : (s + 1) * T].indirect(offs_t[:, lo // 16 : (lo + size) // 16]))
-            for at in range(0, size, P):
-                slot_scales[lo + at, s] = dst[:, at : at + P]
-
-        def gather_words(dst, lo, size, s):
+        for lo, size, s in WORD_RUNS:
+            words = keep.tile([P, size], U32, name=f"words{lo}_{s}", align_bytes=64)
             nc.vector.tensor_copy(
-                dst, xw[:, s * T : (s + 1) * T].bitcast(U32).indirect(offs_t[:, lo // 16 : (lo + size) // 16])
+                words[:], xw[:, s * T : (s + 1) * T].bitcast(U32).indirect(offs_t[:, lo // 16 : (lo + size) // 16])
             )
             for at in range(0, size, P):
-                slot_words[lo + at, s] = dst[:, at : at + P]
+                slot_words[lo + at, s] = words[:, at : at + P]
 
-        pre = {}
         hb = {}
 
-        def first_pass(lo, s):
+        def first_layer(lo):
             e = lo // C
-            if s == 0:
-                pre[lo] = bank(PRE_BANK[lo // P], [P, H])
-            nc.tensor.matmul_mx(
-                out=pre[lo][:],
-                lhsT=slot_words[lo, s].bitcast(FP8X4),
-                lhsT_scale=slot_scales[lo, s],
-                rhs=w1[e][:, s * 2 * H : (s + 1) * 2 * H].bitcast(FP4X4),
-                rhs_scale=w1s[:, (2 * e + s) * H : (2 * e + s + 1) * H],
-                start=(s == 0),
-                stop=(s == 1),
-            )
-
-        def activate(lo):
+            pre = bank(lo // P % 4, [P, H])
+            for s in range(2):
+                at = (2 * e + s) * H
+                nc.tensor.matmul_mx(
+                    out=pre[:],
+                    lhsT=slot_words[lo, s].bitcast(FP8X4),
+                    lhsT_scale=(scales, moved)[s][:, lo : lo + P],
+                    rhs=w1[e][:, s * 2 * H : (s + 1) * 2 * H].bitcast(FP4X4),
+                    rhs_scale=w1s[:, at : at + H],
+                    start=(s == 0),
+                    stop=(s == 1),
+                )
             hb[lo] = keep.tile([P, H], BF16, name=f"hb{lo}")
             nc.scalar.activation(
                 hb[lo][:].rearrange("s (u p d) -> s u p d", u=2, d=2),
-                pre[lo][:].rearrange("s (p u d) -> s u p d", u=2, d=2),
+                pre[:].rearrange("s (p u d) -> s u p d", u=2, d=2),
                 SILU,
             )
 
-        hq = {lo: keep.tile([P, 4 * size], BF16, name=f"hq{lo}", align_bytes=64) for lo, size in GROUPS if lo != C}
-        hq[C] = share.tile([P, 4 * C], BF16, name="hq_late", offset=TOKENS_AT, align_bytes=64)
+        hq = {lo: keep.tile([P, 4 * size], BF16, name=f"hq{lo}", align_bytes=64) for lo, size in GROUPS}
 
         def turn(lo, size, copy, where):
-            group = max(f for f, n in GROUPS if f <= lo)
-            at = lo - group
             blocks = size // P
             hT = bank(where, [P, blocks, 2, P])
             for b in range(blocks):
@@ -164,54 +159,11 @@ def tile_moe_cpy_mlp_silu_kernel(
                 for u in range(2):
                     nc.tensor.transpose(hT[:, b, u, :], pairs[:, u * P : (u + 1) * P], ident[:])
             copy(
-                hq[group][:, 4 * at : 4 * (at + size)].bitcast(F32).rearrange("p (b s u) -> p b s u", b=blocks, u=2),
+                hq[lo][:].bitcast(F32).rearrange("p (b s u) -> p b s u", b=blocks, u=2),
                 hT[:].rearrange("p b u s -> p b s u"),
             )
 
-        scales = keep.tile([P, S], U8, name="scales", align_bytes=64)
-        for s in range(2):
-            gather_scales(scales[:, s * 2 * C : (s + 1) * 2 * C], 0, 2 * C, s)
-        runs = [
-            (0, P, share.tile([P, EXPERT_BYTES // 4], U32, name="words_a", offset=0, align_bytes=64)),
-            (P, P, keep.tile([P, 2 * P], U32, name="words_b", align_bytes=64)),
-            (C, C, share.tile([P, EXPERT_BYTES // 4], U32, name="words_c", offset=EXPERT_BYTES, align_bytes=64)),
-        ]
-        for lo, size, tile in runs:
-            for s in range(2):
-                gather_words(tile[:, s * size : (s + 1) * size], lo, size, s)
-        for lo in range(0, 2 * C, P):
-            for s in range(2):
-                first_pass(lo, s)
-            activate(lo)
-        turn(0, P, nc.scalar.copy, 4)
-        turn(P, P, nc.scalar.copy, 5)
-        turn(C, C, nc.vector.tensor_copy, 0)
-
-        def room(e):
-            at = (e - 2) * EXPERT_BYTES
-            return (
-                share.tile([P, 2 * C], U8, name=f"scales{e}", offset=at, align_bytes=64),
-                share.tile([P, 2 * C], U32, name=f"words{e}", offset=at + 2 * C, align_bytes=64),
-            )
-
-        scales, words = room(2)
-        for s in range(2):
-            gather_scales(scales[:, s * C : (s + 1) * C], 2 * C, C, s)
-            gather_words(words[:, s * C : (s + 1) * C], 2 * C, C, s)
-            for lo in range(2 * C, 3 * C, P):
-                first_pass(lo, s)
-                if s == 1:
-                    activate(lo)
-        scales, words = room(3)
-        for s in range(2):
-            gather_scales(scales[:, s * C : (s + 1) * C], 3 * C, C, s)
-        for b in range(0, C, P):
-            for s in range(2):
-                gather_words(words[:, s * C + b : s * C + b + P], 3 * C + b, P, s)
-                first_pass(3 * C + b, s)
-            activate(3 * C + b)
-
-        codes = share.tile([P, S], U32, name="codes", offset=TOKENS_AT + 4 * S, align_bytes=64)
+        codes = keep.tile([P, S], U32, name="codes", align_bytes=64)
         cs = keep.tile([P, S], U8, name="cs", align_bytes=64)
 
         def quantise(lo, size):
@@ -219,13 +171,19 @@ def tile_moe_cpy_mlp_silu_kernel(
                 out=codes[:, lo : lo + size].bitcast(FP8X4), scales=cs[:, lo : lo + size], in_=hq[lo][:]
             )
 
+        for lo in range(0, 3 * C, P):
+            first_layer(lo)
+        turn(0, C, nc.vector.tensor_copy, 4)
+        turn(C, C, nc.vector.tensor_copy, 5)
+        for lo in range(3 * C, S, P):
+            first_layer(lo)
         quantise(*GROUPS[0])
+        turn(2 * C, C, nc.vector.tensor_copy, 6)
         quantise(*GROUPS[1])
-        turn(2 * C, C, nc.vector.tensor_copy, 3)
-        turn(3 * C, P, nc.scalar.copy, 6)
-        turn(S - P, P, nc.scalar.copy, 7)
-        quantise(*GROUPS[3])
+        turn(3 * C, P, nc.scalar.copy, 7)
+        turn(S - P, P, nc.scalar.copy, 4)
         quantise(*GROUPS[2])
+        quantise(*GROUPS[3])
         quantise(*GROUPS[4])
 
         def second_layer(acc, n, lo, size):
@@ -247,9 +205,9 @@ def tile_moe_cpy_mlp_silu_kernel(
 
         for lo, size, where, copy in (
             (0, 2 * C, 0, nc.scalar.copy),
-            (3 * C, P, 4, nc.vector.tensor_copy),
-            (2 * C, C, 2, nc.scalar.copy),
-            (S - P, P, 5, nc.vector.tensor_copy),
+            (2 * C, C, 1, nc.scalar.copy),
+            (3 * C, P, 2, nc.vector.tensor_copy),
+            (S - P, P, 3, nc.vector.tensor_copy),
         ):
             acc = bank(where, [P, size])
             second_layer(acc, 0, lo, size)

@@ -23,7 +23,7 @@ ADD = mybir.AluOpType.add
 SILU = mybir.ActivationFunctionType.Silu
 
 HALF = T // 2
-AHEAD = 4
+AHEAD = 5
 RING = 4
 
 SHIFT = 16
@@ -213,9 +213,9 @@ def tile_moe_cpy_mlp_silu_kernel(
             second_layer(acc, 0, lo, size)
             copy(y[0][:, lo : lo + size], acc[:])
 
-        def slots_of(n):
+        def slots_of(n, first_bank):
             for lo in range(0, S, 2 * C):
-                acc = bank(6 + lo // (2 * C), [P, 2 * C])
+                acc = bank(first_bank + lo // (2 * C), [P, 2 * C])
                 second_layer(acc, n, lo, 2 * C)
                 nc.scalar.copy(y[n][:, lo : lo + 2 * C], acc[:])
 
@@ -229,26 +229,26 @@ def tile_moe_cpy_mlp_silu_kernel(
         LAST_TURNED = NB - 2
 
         def turn_and_add(n):
+            first = weighted(n, 0, 0, T)
+            sumT = [bank(2 * (n % 2) + i, [P, HALF]) for i in range(2)]
+            for j in range(0, T, P):
+                i, col = divmod(j, HALF)
+                nc.tensor.matmul(
+                    sumT[i][:, col : col + P], first[:, j : j + P], ident[:],
+                    start=(col == 0), stop=False, is_transpose=True,
+                )
             if n < LAST_TURNED:
-                whole = [weighted(n, r, 0, T) for r in range(2)]
+                whole = weighted(n, 1, 0, T)
             turned = []
             for at in range(0, T, HALF):
-                if n < LAST_TURNED:
-                    a = [whole[r][:, at : at + HALF] for r in range(2)]
-                else:
-                    a = [weighted(n, r, at, HALF)[:] for r in range(2)]
-                sumT = bank(2 * (n % 2) + at // HALF, [P, HALF])
+                second = whole[:, at : at + HALF] if n < LAST_TURNED else weighted(n, 1, at, HALF)[:]
                 for j in range(0, HALF, P):
-                    for r in range(2):
-                        nc.tensor.matmul(
-                            sumT[:, j : j + P], a[r][:, j : j + P], ident[:],
-                            start=(r == 0), stop=(r == 1), is_transpose=True,
-                        )
-                if n == LAST_TURNED:
-                    t = keep.tile([P, HALF], F32, name="turned", tag=f"last{at}")
-                else:
-                    t = keep.tile([P, HALF], F32, name="turned", bufs=RING)
-                nc.scalar.copy(t[:], sumT[:])
+                    nc.tensor.matmul(
+                        sumT[at // HALF][:, j : j + P], second[:, j : j + P], ident[:],
+                        start=False, stop=(j == HALF - P), is_transpose=True,
+                    )
+                t = keep.tile([P, HALF], F32, name="turned", bufs=RING)
+                nc.scalar.copy(t[:], sumT[at // HALF][:])
                 turned.append(t)
             return turned
 
@@ -261,24 +261,22 @@ def tile_moe_cpy_mlp_silu_kernel(
                 cols = slice(i * HALF, (i + 1) * HALF)
                 nc.scalar.copy(res[:, cols], back[:])
                 if n == LAST_TURNED:
-                    nc.sync.dma_start(out[n * P : (n + 1) * P, cols], res[:, cols])
+                    nc.scalar.dma_start(out[n * P : (n + 1) * P, cols], res[:, cols])
             if n != LAST_TURNED:
-                nc.sync.dma_start(out[n * P : (n + 1) * P, :], res[:])
+                nc.scalar.dma_start(out[n * P : (n + 1) * P, :], res[:])
 
-        for n in range(1, AHEAD):
-            slots_of(n)
+        for n, first_bank in zip(range(1, AHEAD), (6, 4, 0, 2)):
+            slots_of(n, first_bank)
         for n in range(LAST_TURNED + 1):
             turned = turn_and_add(n)
-            if AHEAD + 2 * n < NB:
-                slots_of(AHEAD + 2 * n)
+            if AHEAD + n < NB:
+                slots_of(AHEAD + n, 6)
             turn_back(n, turned)
-            if AHEAD + 2 * n + 1 < NB:
-                slots_of(AHEAD + 2 * n + 1)
 
         n = NB - 1
         first = weighted(n, 0, 0, T)
         second = [weighted(n, 1, at, HALF) for at in range(0, T, HALF)]
         for at in range(0, T, HALF):
-            res_last = keep.tile([P, HALF], F32, name="res_last", tag=f"last{at}")
+            res_last = keep.tile([P, HALF], F32, name=f"res_last{at}")
             nc.vector.tensor_tensor(res_last[:], first[:, at : at + HALF], second[at // HALF][:], ADD)
             nc.sync.dma_start(out[n * P : (n + 1) * P, at : at + HALF], res_last[:])

@@ -21,10 +21,12 @@ FP4X4 = mybir.dt.float4_e2m1fn_x4
 MULT = mybir.AluOpType.mult
 ADD = mybir.AluOpType.add
 SILU = mybir.ActivationFunctionType.Silu
+COPY = mybir.ActivationFunctionType.Copy
 
-HALF = T // 2
-AHEAD = 5
-RING = 4
+TV = 512
+TS = T - TV
+CH = TS // P
+PAIRS = [(0, 1), (2, 3), (4, 5), (6, 7)]
 
 SHIFT = 16
 W1_LOADS = [(0, 1), (1, 1), (2, 2)]
@@ -59,7 +61,8 @@ def tile_moe_cpy_mlp_silu_kernel(
         w2s = keep.tile([P, E * K], U8, name="w2s", align_bytes=64)
         y = [keep.tile([P, W], F32, name=f"y{n}") for n in range(NB)]
         ident = keep.tile([P, P], F32, name="ident")
-        g = keep.tile([P, 2, T], F32, name="g")
+        g = keep.tile([P, 2, TV], F32, name="g")
+        gT = [keep.tile([P, CH], F32, name=f"gT{r}") for r in range(2)]
 
         nc.gpsimd.memset(xs[:].bitcast(I32), 0)
         nc.vector.memset(w1s[:].bitcast(I32), 0)
@@ -111,9 +114,12 @@ def tile_moe_cpy_mlp_silu_kernel(
         load_scale_rows(w2s, w2_scales.bitcast(I32).rearrange("e s b n -> b (e s) n"), (nc.sync,))
         load_w2(0)
         load_xr(0)
-        nc.sync.dma_start(g[:], gate.rearrange("r p t -> p r t"))
+        nc.sync.dma_start(g[:], gate.rearrange("r p t -> p r t")[:, :, 0:TV])
         load_xr(1)
         load_w2(1)
+        with nc.allow_non_contiguous_dma(reason="one gate value a token and partition"):
+            for r in range(2):
+                nc.sync.dma_start(gT[r][:], gate[r, 0, TV:T].rearrange("(c p) -> p c", p=P))
         for n in range(2, NB):
             load_xr(n)
 
@@ -219,6 +225,9 @@ def tile_moe_cpy_mlp_silu_kernel(
                 second_layer(acc, n, lo, 2 * C)
                 nc.scalar.copy(y[n][:, lo : lo + 2 * C], acc[:])
 
+        for n, first_bank in zip(range(1, NB), (6, 4, 0, 2, 6, 4, 0)):
+            slots_of(n, first_bank)
+
         def weighted(n, r, lo, size):
             a = keep.tile([P, size], F32, name=f"a{n}_{r}_{lo}")
             nc.vector.tensor_tensor(
@@ -226,57 +235,69 @@ def tile_moe_cpy_mlp_silu_kernel(
             )
             return a
 
-        LAST_TURNED = NB - 2
+        def add_and_store(n, first, second, lo, size):
+            res = keep.tile([P, size], F32, name=f"res{n}_{lo}")
+            nc.vector.tensor_tensor(res[:], first, second, ADD)
+            nc.sync.dma_start(out[n * P : (n + 1) * P, lo : lo + size], res[:])
 
-        def turn_and_add(n):
-            first = weighted(n, 0, 0, T)
-            sumT = [bank(2 * (n % 2) + i, [P, HALF]) for i in range(2)]
-            for j in range(0, T, P):
-                i, col = divmod(j, HALF)
-                nc.tensor.matmul(
-                    sumT[i][:, col : col + P], first[:, j : j + P], ident[:],
-                    start=(col == 0), stop=False, is_transpose=True,
-                )
-            if n < LAST_TURNED:
-                whole = weighted(n, 1, 0, T)
+        first = weighted(0, 0, 0, TV)
+        for n in range(NB - 1):
+            second = weighted(n, 1, 0, TV)
+            coming = weighted(n + 1, 0, 0, TV)
+            add_and_store(n, first[:], second[:], 0, TV)
+            first = coming
+        halves = [weighted(NB - 1, 1, lo, TV // 2) for lo in (0, TV // 2)]
+        for i, lo in enumerate((0, TV // 2)):
+            add_and_store(NB - 1, first[:, lo : lo + TV // 2], halves[i][:], lo, TV // 2)
+
+        def fetch(k):
+            blocks = PAIRS[k]
+            got = keep.tile([P, 2, len(blocks), TS], F32, name=f"got{k}")
             turned = []
-            for at in range(0, T, HALF):
-                second = whole[:, at : at + HALF] if n < LAST_TURNED else weighted(n, 1, at, HALF)[:]
-                for j in range(0, HALF, P):
-                    nc.tensor.matmul(
-                        sumT[at // HALF][:, j : j + P], second[:, j : j + P], ident[:],
-                        start=False, stop=(j == HALF - P), is_transpose=True,
-                    )
-                t = keep.tile([P, HALF], F32, name="turned", bufs=RING)
-                nc.scalar.copy(t[:], sumT[at // HALF][:])
-                turned.append(t)
+            for r in range(2):
+                for b, n in enumerate(blocks):
+                    nc.scalar.activation(got[:, r, b, :], y[n][:].indirect(pos_t[r][:, TV // 16 : T // 16]), COPY)
+                tT = bank((2, 6, 0)[k % 3] + r, [P, CH, len(blocks), P])
+                for c in range(CH):
+                    for b in range(len(blocks)):
+                        nc.tensor.transpose(tT[:, c, b, :], got[:, r, b, c * P : (c + 1) * P], ident[:])
+                turned.append(tT)
             return turned
 
-        def turn_back(n, turned):
-            res = keep.tile([P, T], F32, name="res", bufs=RING)
-            for i, t in enumerate(turned):
-                back = bank(4 + i, [P, HALF])
-                for j in range(0, HALF, P):
-                    nc.tensor.transpose(back[:, j : j + P], t[:, j : j + P], ident[:])
-                cols = slice(i * HALF, (i + 1) * HALF)
-                nc.scalar.copy(res[:, cols], back[:])
-                if n == LAST_TURNED:
-                    nc.scalar.dma_start(out[n * P : (n + 1) * P, cols], res[:, cols])
-            if n != LAST_TURNED:
-                nc.scalar.dma_start(out[n * P : (n + 1) * P, :], res[:])
+        def weigh(k, turned):
+            blocks = PAIRS[k]
+            u = keep.tile([P, 2, CH, len(blocks), P], F32, name=f"u{k}")
+            back = bank(4 + k % 2, [P, len(blocks), TS])
+            for r in range(2):
+                for c in range(CH):
+                    nc.scalar.activation(
+                        u[:, r, c].rearrange("p b n -> p (b n)"),
+                        turned[r][:, c].rearrange("p b n -> p (b n)"),
+                        COPY,
+                        scale=gT[r][:, c : c + 1],
+                    )
+                    for b in range(len(blocks)):
+                        nc.tensor.matmul(
+                            back[:, b, c * P : (c + 1) * P], u[:, r, c, b, :], ident[:],
+                            start=(r == 0 and c == 0 and b == 0),
+                            stop=(r == 1 and c == CH - 1 and b == len(blocks) - 1),
+                            is_transpose=True,
+                        )
+            return back
 
-        for n, first_bank in zip(range(1, AHEAD), (6, 4, 0, 2)):
-            slots_of(n, first_bank)
-        for n in range(LAST_TURNED + 1):
-            turned = turn_and_add(n)
-            if AHEAD + n < NB:
-                slots_of(AHEAD + n, 6)
-            turn_back(n, turned)
+        def leave(k, back):
+            blocks = PAIRS[k]
+            res = keep.tile([P, len(blocks), TS], F32, name=f"left{k}")
+            nc.scalar.copy(res[:], back[:])
+            rows = out[blocks[0] * P : (blocks[-1] + 1) * P, TV:T]
+            nc.scalar.dma_start(rows.rearrange("(b p) t -> p b t", p=P), res[:])
 
-        n = NB - 1
-        first = weighted(n, 0, 0, T)
-        second = [weighted(n, 1, at, HALF) for at in range(0, T, HALF)]
-        for at in range(0, T, HALF):
-            res_last = keep.tile([P, HALF], F32, name=f"res_last{at}")
-            nc.vector.tensor_tensor(res_last[:], first[:, at : at + HALF], second[at // HALF][:], ADD)
-            nc.sync.dma_start(out[n * P : (n + 1) * P, at : at + HALF], res_last[:])
+        turned = {0: fetch(0)}
+        backs = {}
+        for k in range(len(PAIRS)):
+            if k + 1 < len(PAIRS):
+                turned[k + 1] = fetch(k + 1)
+            if k > 0:
+                leave(k - 1, backs[k - 1])
+            backs[k] = weigh(k, turned[k])
+        leave(len(PAIRS) - 1, backs[len(PAIRS) - 1])

@@ -26,7 +26,8 @@ COPY = mybir.ActivationFunctionType.Copy
 TV = 512
 TS = T - TV
 CH = TS // P
-PAIRS = [(0, 1), (2, 3), (4, 5), (6, 7)]
+PAIRS = [((0, 1), 0), ((2, 3), 0), ((4, 5), 0), ((6, 7), 1)]
+TG = TV + P
 
 SHIFT = 16
 W1_LOADS = [(0, 1), (1, 1), (2, 2)]
@@ -61,7 +62,7 @@ def tile_moe_cpy_mlp_silu_kernel(
         w2s = keep.tile([P, E * K], U8, name="w2s", align_bytes=64)
         y = [keep.tile([P, W], F32, name=f"y{n}") for n in range(NB)]
         ident = keep.tile([P, P], F32, name="ident")
-        g = keep.tile([P, 2, TV], F32, name="g")
+        g = keep.tile([P, 2, TG], F32, name="g")
         gT = [keep.tile([P, CH], F32, name=f"gT{r}") for r in range(2)]
 
         nc.gpsimd.memset(xs[:].bitcast(I32), 0)
@@ -114,7 +115,7 @@ def tile_moe_cpy_mlp_silu_kernel(
         load_scale_rows(w2s, w2_scales.bitcast(I32).rearrange("e s b n -> b (e s) n"), (nc.sync,))
         load_w2(0)
         load_xr(0)
-        nc.sync.dma_start(g[:], gate.rearrange("r p t -> p r t")[:, :, 0:TV])
+        nc.sync.dma_start(g[:], gate.rearrange("r p t -> p r t")[:, :, 0:TG])
         load_xr(1)
         load_w2(1)
         with nc.allow_non_contiguous_dma(reason="one gate value a token and partition"):
@@ -240,56 +241,61 @@ def tile_moe_cpy_mlp_silu_kernel(
             nc.vector.tensor_tensor(res[:], first, second, ADD)
             nc.sync.dma_start(out[n * P : (n + 1) * P, lo : lo + size], res[:])
 
-        first = weighted(0, 0, 0, TV)
+        mine = {n: TV + c0 * P for blocks, c0 in PAIRS for n in blocks}
+        first = weighted(0, 0, 0, mine[0])
         for n in range(NB - 1):
-            second = weighted(n, 1, 0, TV)
-            coming = weighted(n + 1, 0, 0, TV)
-            add_and_store(n, first[:], second[:], 0, TV)
+            second = weighted(n, 1, 0, mine[n])
+            coming = weighted(n + 1, 0, 0, mine[n + 1])
+            add_and_store(n, first[:], second[:], 0, mine[n])
             first = coming
-        halves = [weighted(NB - 1, 1, lo, TV // 2) for lo in (0, TV // 2)]
-        for i, lo in enumerate((0, TV // 2)):
-            add_and_store(NB - 1, first[:, lo : lo + TV // 2], halves[i][:], lo, TV // 2)
+        half = mine[NB - 1] // 2
+        halves = [weighted(NB - 1, 1, lo, half) for lo in (0, half)]
+        for i, lo in enumerate((0, half)):
+            add_and_store(NB - 1, first[:, lo : lo + half], halves[i][:], lo, half)
 
         def fetch(k):
-            blocks = PAIRS[k]
-            got = keep.tile([P, 2, len(blocks), TS], F32, name=f"got{k}")
+            blocks, c0 = PAIRS[k]
+            lo = TV + c0 * P
+            got = keep.tile([P, 2, len(blocks), T - lo], F32, name=f"got{k}")
             turned = []
             for r in range(2):
                 for b, n in enumerate(blocks):
-                    nc.scalar.activation(got[:, r, b, :], y[n][:].indirect(pos_t[r][:, TV // 16 : T // 16]), COPY)
-                tT = bank((2, 6, 0)[k % 3] + r, [P, CH, len(blocks), P])
-                for c in range(CH):
+                    nc.scalar.activation(got[:, r, b, :], y[n][:].indirect(pos_t[r][:, lo // 16 : T // 16]), COPY)
+                tT = bank((2, 6, 0)[k % 3] + r, [P, CH - c0, len(blocks), P])
+                for c in range(CH - c0):
                     for b in range(len(blocks)):
                         nc.tensor.transpose(tT[:, c, b, :], got[:, r, b, c * P : (c + 1) * P], ident[:])
                 turned.append(tT)
             return turned
 
         def weigh(k, turned):
-            blocks = PAIRS[k]
-            u = keep.tile([P, 2, CH, len(blocks), P], F32, name=f"u{k}")
-            back = bank(4 + k % 2, [P, len(blocks), TS])
+            blocks, c0 = PAIRS[k]
+            chunks = CH - c0
+            u = keep.tile([P, 2, chunks, len(blocks), P], F32, name=f"u{k}")
+            back = bank(4 + k % 2, [P, len(blocks), chunks * P])
             for r in range(2):
-                for c in range(CH):
+                for c in range(chunks):
                     nc.scalar.activation(
                         u[:, r, c].rearrange("p b n -> p (b n)"),
                         turned[r][:, c].rearrange("p b n -> p (b n)"),
                         COPY,
-                        scale=gT[r][:, c : c + 1],
+                        scale=gT[r][:, c0 + c : c0 + c + 1],
                     )
                     for b in range(len(blocks)):
                         nc.tensor.matmul(
                             back[:, b, c * P : (c + 1) * P], u[:, r, c, b, :], ident[:],
                             start=(r == 0 and c == 0 and b == 0),
-                            stop=(r == 1 and c == CH - 1 and b == len(blocks) - 1),
+                            stop=(r == 1 and c == chunks - 1 and b == len(blocks) - 1),
                             is_transpose=True,
                         )
             return back
 
         def leave(k, back):
-            blocks = PAIRS[k]
-            res = keep.tile([P, len(blocks), TS], F32, name=f"left{k}")
+            blocks, c0 = PAIRS[k]
+            lo = TV + c0 * P
+            res = keep.tile([P, len(blocks), T - lo], F32, name=f"left{k}")
             nc.scalar.copy(res[:], back[:])
-            rows = out[blocks[0] * P : (blocks[-1] + 1) * P, TV:T]
+            rows = out[blocks[0] * P : (blocks[-1] + 1) * P, lo:T]
             nc.scalar.dma_start(rows.rearrange("(b p) t -> p b t", p=P), res[:])
 
         turned = {0: fetch(0)}

@@ -26,14 +26,12 @@ COPY = mybir.ActivationFunctionType.Copy
 TV = 512
 TS = T - TV
 CH = TS // P
-PAIRS = [((0, 1), 0), ((2, 3), 0), ((4, 5), 0), ((6, 7), 1)]
+PAIRS = [((0, 1), 0), ((2, 3), 0), ((4, 5), 0), ((6,), 0), ((7,), 1)]
 TG = TV + P
 
 SHIFT = 16
 W1_LOADS = [(0, 1), (1, 1), (2, 2)]
 GROUPS = [(0, C), (C, C), (2 * C, C), (3 * C, P), (S - P, P)]
-WORD_RUNS = [(0, P, 0), (0, P, 1), (P, P, 0), (P, P, 1), (C, C, 0), (C, C, 1), (2 * C, C, 0), (2 * C, C, 1),
-             (3 * C, C, 0), (3 * C, P, 1), (S - P, P, 1)]
 
 
 def tile_moe_cpy_mlp_silu_kernel(
@@ -55,8 +53,13 @@ def tile_moe_cpy_mlp_silu_kernel(
         xs = keep.tile([P, T], U8, name="xs", align_bytes=64)
         scales = keep.tile([P, S], U8, name="scales", align_bytes=64)
         moved = keep.tile([P, S], U8, name="moved", align_bytes=64)
-        w1_tiles = {e0: keep.tile([P, n * 4 * H], U8, name=f"w1_{e0}", align_bytes=64) for e0, n in W1_LOADS}
-        w1 = [w1_tiles[e0][:, j * 4 * H : (j + 1) * 4 * H] for e0, n in W1_LOADS for j in range(n)]
+        w1_tiles = {
+            e0: keep.tile([P, n * 4 * H], U8, name=f"w1_{e0}", tag=f"raw{e0}", align_bytes=64) for e0, n in W1_LOADS
+        }
+        w1 = {e0 + j: w1_tiles[e0][:, j * 4 * H : (j + 1) * 4 * H] for e0, n in W1_LOADS for j in range(n)}
+        w1p_tiles = {e0: keep.tile([P, n * 4 * H], U8, name=f"w1p{e0}", align_bytes=64) for e0, n in W1_LOADS[1:]}
+        w1p = {e0 + j: w1p_tiles[e0][:, j * 4 * H : (j + 1) * 4 * H] for e0, n in W1_LOADS[1:] for j in range(n)}
+        w1ps = {e: keep.tile([P, 2 * H], U8, name=f"w1ps{e}", align_bytes=64) for e in range(1, E)}
         w1s = keep.tile([P, E * 2 * H], U8, name="w1s", align_bytes=64)
         w2 = [keep.tile([P, E * K], U8, name=f"w2_{h}", align_bytes=64) for h in range(2)]
         w2s = keep.tile([P, E * K], U8, name="w2s", align_bytes=64)
@@ -124,74 +127,103 @@ def tile_moe_cpy_mlp_silu_kernel(
         for n in range(2, NB):
             load_xr(n)
 
-        slot_words = {}
-        for lo, size, s in WORD_RUNS:
-            words = keep.tile([P, size], U32, name=f"words{lo}_{s}", align_bytes=64)
-            nc.vector.tensor_copy(
-                words[:], xw[:, s * T : (s + 1) * T].bitcast(U32).indirect(offs_t[:, lo // 16 : (lo + size) // 16])
-            )
-            for at in range(0, size, P):
-                slot_words[lo + at, s] = words[:, at : at + P]
-
-        hb = {}
-
-        def first_layer(lo):
-            e = lo // C
-            pre = bank(lo // P % 4, [P, H])
-            for s in range(2):
-                at = (2 * e + s) * H
-                nc.tensor.matmul_mx(
-                    out=pre[:],
-                    lhsT=slot_words[lo, s].bitcast(FP8X4),
-                    lhsT_scale=(scales, moved)[s][:, lo : lo + P],
-                    rhs=w1[e][:, s * 2 * H : (s + 1) * 2 * H].bitcast(FP4X4),
-                    rhs_scale=w1s[:, at : at + H],
-                    start=(s == 0),
-                    stop=(s == 1),
-                )
-            hb[lo] = keep.tile([P, H], BF16, name=f"hb{lo}")
-            nc.scalar.activation(
-                hb[lo][:].rearrange("s (u p d) -> s u p d", u=2, d=2),
-                pre[:].rearrange("s (p u d) -> s u p d", u=2, d=2),
-                SILU,
+        for e in range(1, E):
+            nc.gpsimd.tensor_copy(
+                w1ps[e][:].rearrange("p (s t m) -> p s t m", s=2, t=4),
+                w1s[:, 2 * e * H : 2 * (e + 1) * H].rearrange("p (s m t) -> p s t m", s=2, t=4),
             )
 
-        hq = {lo: keep.tile([P, 4 * size], BF16, name=f"hq{lo}", align_bytes=64) for lo, size in GROUPS}
-
-        def turn(lo, size, copy, where):
-            blocks = size // P
-            hT = bank(where, [P, blocks, 2, P])
-            for b in range(blocks):
-                pairs = hb[lo + b * P][:].bitcast(F32)
-                for u in range(2):
-                    nc.tensor.transpose(hT[:, b, u, :], pairs[:, u * P : (u + 1) * P], ident[:])
+        def order_words(e0, copy):
             copy(
-                hq[lo][:].bitcast(F32).rearrange("p (b s u) -> p b s u", b=blocks, u=2),
-                hT[:].rearrange("p b u s -> p b s u"),
+                w1p_tiles[e0][:].bitcast(U16).rearrange("p (a t m) -> p a t m", t=4, m=P),
+                w1_tiles[e0][:].bitcast(U16).rearrange("p (a m t) -> p a t m", t=4, m=P),
             )
 
+        slot_words = {}
+
+        def gather_words(first, slots, runs, tag):
+            words = keep.tile([P, 2 * slots], U32, name=f"words{first}", tag=tag, align_bytes=64)
+            for at, size, s in runs:
+                lo = first + at
+                nc.vector.tensor_copy(
+                    words[:, s * slots + at : s * slots + at + size],
+                    xw[:, s * T : (s + 1) * T].bitcast(U32).indirect(offs_t[:, lo // 16 : (lo + size) // 16]),
+                )
+            for at in range(0, slots, P):
+                for s in range(2):
+                    slot_words[first + at, s] = words[:, s * slots + at : s * slots + at + P]
+
+        gather_words(0, C, [(0, P, 0), (0, P, 1), (P, P, 0), (P, P, 1)], "words0")
+        order_words(1, nc.scalar.copy)
+        gather_words(C, C, [(0, C, 0), (0, C, 1)], "words1")
+        order_words(2, nc.vector.tensor_copy)
+        gather_words(2 * C, 2 * C, [(at, P, s) for at in range(0, 2 * C, P) for s in range(2)], "raw2")
+
+        hq = keep.tile([P, 4 * S], BF16, name="hq", align_bytes=64)
         codes = keep.tile([P, S], U32, name="codes", align_bytes=64)
         cs = keep.tile([P, S], U8, name="cs", align_bytes=64)
 
         def quantise(lo, size):
             nc.vector.quantize_mx(
-                out=codes[:, lo : lo + size].bitcast(FP8X4), scales=cs[:, lo : lo + size], in_=hq[lo][:]
+                out=codes[:, lo : lo + size].bitcast(FP8X4),
+                scales=cs[:, lo : lo + size],
+                in_=hq[:, 4 * lo : 4 * (lo + size)],
             )
 
-        for lo in range(0, 3 * C, P):
+        def first_layer(lo):
+            e = lo // C
+            pre = bank(lo // P, [P, 4, P])
+            for s in range(2):
+                for t in range(4):
+                    at = s * H + t * P
+                    nc.tensor.matmul_mx(
+                        out=pre[:, t, :],
+                        lhsT=w1p[e][:, 2 * at : 2 * (at + P)].bitcast(FP4X4),
+                        lhsT_scale=w1ps[e][:, at : at + P],
+                        rhs=slot_words[lo, s].bitcast(FP8X4),
+                        rhs_scale=(scales, moved)[s][:, lo : lo + P],
+                        start=(s == 0 and t == 0),
+                        stop=(s == 1 and t == 3),
+                    )
+            nc.scalar.activation(
+                hq[:, 4 * lo : 4 * (lo + P)].rearrange("p (s t) -> p s t", t=4),
+                pre[:].rearrange("p t s -> p s t"),
+                SILU,
+            )
+
+        hb = keep.tile([P, 2, H], BF16, name="hb")
+        for b in range(2):
+            pre = bank(b, [P, H])
+            for s in range(2):
+                nc.tensor.matmul_mx(
+                    out=pre[:],
+                    lhsT=slot_words[b * P, s].bitcast(FP8X4),
+                    lhsT_scale=(scales, moved)[s][:, b * P : (b + 1) * P],
+                    rhs=w1[0][:, s * 2 * H : (s + 1) * 2 * H].bitcast(FP4X4),
+                    rhs_scale=w1s[:, s * H : (s + 1) * H],
+                    start=(s == 0),
+                    stop=(s == 1),
+                )
+            nc.scalar.activation(
+                hb[:, b, :].rearrange("s (u p d) -> s u p d", u=2, d=2),
+                pre[:].rearrange("s (p u d) -> s u p d", u=2, d=2),
+                SILU,
+            )
+        for lo in range(C, 2 * C, P):
             first_layer(lo)
-        turn(0, C, nc.vector.tensor_copy, 4)
-        turn(C, C, nc.vector.tensor_copy, 5)
-        for lo in range(3 * C, S, P):
+        hT = bank(0, [P, 2, 2, P])
+        for b in range(2):
+            pairs = hb[:, b, :].bitcast(F32)
+            for u in range(2):
+                nc.tensor.transpose(hT[:, b, u, :], pairs[:, u * P : (u + 1) * P], ident[:])
+        nc.scalar.copy(
+            hq[:, 0 : 4 * C].bitcast(F32).rearrange("p (b s u) -> p b s u", b=2, u=2),
+            hT[:].rearrange("p b u s -> p b s u"),
+        )
+        for lo in range(2 * C, S, P):
             first_layer(lo)
-        quantise(*GROUPS[0])
-        turn(2 * C, C, nc.vector.tensor_copy, 6)
-        quantise(*GROUPS[1])
-        turn(3 * C, P, nc.scalar.copy, 7)
-        turn(S - P, P, nc.scalar.copy, 4)
-        quantise(*GROUPS[2])
-        quantise(*GROUPS[3])
-        quantise(*GROUPS[4])
+        for i in (1, 0, 2, 3, 4):
+            quantise(*GROUPS[i])
 
         def second_layer(acc, n, lo, size):
             h, m = divmod(n, NB // 2)
@@ -211,10 +243,9 @@ def tile_moe_cpy_mlp_silu_kernel(
                 done = done + run
 
         for lo, size, where, copy in (
-            (0, 2 * C, 0, nc.scalar.copy),
-            (2 * C, C, 1, nc.scalar.copy),
-            (3 * C, P, 2, nc.vector.tensor_copy),
-            (S - P, P, 3, nc.vector.tensor_copy),
+            (0, 2 * C, 1, nc.scalar.copy),
+            (2 * C, C, 2, nc.vector.tensor_copy),
+            (3 * C, C, 3, nc.scalar.copy),
         ):
             acc = bank(where, [P, size])
             second_layer(acc, 0, lo, size)
@@ -226,7 +257,7 @@ def tile_moe_cpy_mlp_silu_kernel(
                 second_layer(acc, n, lo, 2 * C)
                 nc.scalar.copy(y[n][:, lo : lo + 2 * C], acc[:])
 
-        for n, first_bank in zip(range(1, NB), (6, 4, 0, 2, 6, 4, 0)):
+        for n, first_bank in zip(range(1, NB), (4, 6, 0, 2, 4, 6, 0)):
             slots_of(n, first_bank)
 
         def weighted(n, r, lo, size):

@@ -41,6 +41,7 @@ def tile_moe_cpy_mlp_silu_kernel(
     with ExitStack() as ctx:
         lists = ctx.enter_context(tc.tile_pool(name="lists", bufs=1))
         keep = ctx.enter_context(tc.tile_pool(name="keep", bufs=1))
+        reuse = ctx.enter_context(tc.tile_pool(name="reuse", bufs=1))
         psum = ctx.enter_context(tc.psum_pool(name="psum", bufs=1))
 
         def bank(i, shape):
@@ -49,17 +50,16 @@ def tile_moe_cpy_mlp_silu_kernel(
         offs_t = lists.tile([P, S // 16], U16, name="offs_t")
         pos_t = [lists.tile([P, T // 16], U16, name=f"pos_t{r}") for r in range(2)]
 
-        xw = keep.tile([P, 2 * T], I32, name="xw", align_bytes=64)
+        xw = [keep.tile([P, T], I32, name=f"xw{s}", align_bytes=64) for s in range(2)]
         xs = keep.tile([P, T], U8, name="xs", align_bytes=64)
         scales = keep.tile([P, S], U8, name="scales", align_bytes=64)
         moved = keep.tile([P, S], U8, name="moved", align_bytes=64)
-        w1_tiles = {
-            e0: keep.tile([P, n * 4 * H], U8, name=f"w1_{e0}", tag=f"raw{e0}", align_bytes=64) for e0, n in W1_LOADS
-        }
+        w1_tiles = {e: keep.tile([P, 4 * H], U8, name=f"w1_{e}", align_bytes=64) for e in range(2)}
+        w1_tiles[2] = reuse.tile([P, 8 * H], U8, name="w1_2", offset=0, align_bytes=64)
         w1 = {e0 + j: w1_tiles[e0][:, j * 4 * H : (j + 1) * 4 * H] for e0, n in W1_LOADS for j in range(n)}
         w1p_tiles = {e0: keep.tile([P, n * 4 * H], U8, name=f"w1p{e0}", align_bytes=64) for e0, n in W1_LOADS[1:]}
         w1p = {e0 + j: w1p_tiles[e0][:, j * 4 * H : (j + 1) * 4 * H] for e0, n in W1_LOADS[1:] for j in range(n)}
-        w1ps = {e: keep.tile([P, 2 * H], U8, name=f"w1ps{e}", align_bytes=64) for e in range(1, E)}
+        w1ps = {e: keep.tile([P, 2 * H], U8, name=f"w1ps{e}", align_bytes=64) for e in (1, 2)}
         w1s = keep.tile([P, E * 2 * H], U8, name="w1s", align_bytes=64)
         w2 = [keep.tile([P, E * K], U8, name=f"w2_{h}", align_bytes=64) for h in range(2)]
         w2s = keep.tile([P, E * K], U8, name="w2s", align_bytes=64)
@@ -103,12 +103,12 @@ def tile_moe_cpy_mlp_silu_kernel(
         xs_rows = x_scales.bitcast(I32).rearrange("s b t -> b s t")
         for r in range(4):
             (nc.sync, nc.scalar)[r % 2].dma_start(xs[r:P:SHIFT, :].bitcast(I32), xs_rows[r:16:4])
-        nc.sync.dma_start(
-            xw[:].rearrange("p (s t) -> p s t", s=2), x_words.rearrange("s p t d -> p s (t d)").bitcast(I32)
-        )
+        token_words = x_words.rearrange("s p t d -> s p (t d)").bitcast(I32)
+        nc.sync.dma_start(xw[0][:], token_words[0])
         load_scale_rows(w1s, w1_scales.bitcast(I32).rearrange("e s b i -> b (e s) i"), (nc.sync,))
         load_w1(*W1_LOADS[0])
         load_w1(*W1_LOADS[1])
+        nc.sync.dma_start(xw[1][:], token_words[1])
         load_w1(*W1_LOADS[2])
         for lo, hi, queue in ((0, C, nc.scalar), (C, 2 * C, nc.scalar), (2 * C, S, nc.sync)):
             nc.vector.tensor_copy(scales[:, lo:hi], xs[:].indirect(offs_t[:, lo // 16 : hi // 16]))
@@ -127,7 +127,7 @@ def tile_moe_cpy_mlp_silu_kernel(
         for n in range(2, NB):
             load_xr(n)
 
-        for e in range(1, E):
+        def order_scales(e):
             nc.gpsimd.tensor_copy(
                 w1ps[e][:].rearrange("p (s t m) -> p s t m", s=2, t=4),
                 w1s[:, 2 * e * H : 2 * (e + 1) * H].rearrange("p (s m t) -> p s t m", s=2, t=4),
@@ -141,23 +141,27 @@ def tile_moe_cpy_mlp_silu_kernel(
 
         slot_words = {}
 
-        def gather_words(first, slots, runs, tag):
-            words = keep.tile([P, 2 * slots], U32, name=f"words{first}", tag=tag, align_bytes=64)
+        def gather_words(words, first, slots, runs):
             for at, size, s in runs:
                 lo = first + at
                 nc.vector.tensor_copy(
                     words[:, s * slots + at : s * slots + at + size],
-                    xw[:, s * T : (s + 1) * T].bitcast(U32).indirect(offs_t[:, lo // 16 : (lo + size) // 16]),
+                    xw[s][:].bitcast(U32).indirect(offs_t[:, lo // 16 : (lo + size) // 16]),
                 )
             for at in range(0, slots, P):
                 for s in range(2):
                     slot_words[first + at, s] = words[:, s * slots + at : s * slots + at + P]
 
-        gather_words(0, C, [(0, P, 0), (0, P, 1), (P, P, 0), (P, P, 1)], "words0")
+        order_scales(1)
+        order_scales(2)
         order_words(1, nc.scalar.copy)
-        gather_words(C, C, [(0, C, 0), (0, C, 1)], "words1")
+        early = keep.tile([P, 4 * C], U32, name="early", align_bytes=64)
+        gather_words(early, 0, 2 * C, [(at, size, s) for s in range(2) for at, size in ((0, P), (P, P), (C, C))])
         order_words(2, nc.vector.tensor_copy)
-        gather_words(2 * C, 2 * C, [(at, P, s) for at in range(0, 2 * C, P) for s in range(2)], "raw2")
+        w1ps[3] = reuse.tile([P, 2 * H], U8, name="w1ps3", offset=0, align_bytes=64)
+        order_scales(3)
+        late = reuse.tile([P, 4 * C], U32, name="late", offset=2 * H, align_bytes=64)
+        gather_words(late, 2 * C, 2 * C, [(at, P, s) for at in range(0, 2 * C, P) for s in range(2)])
 
         hq = keep.tile([P, 4 * S], BF16, name="hq", align_bytes=64)
         codes = keep.tile([P, S], U32, name="codes", align_bytes=64)
@@ -244,8 +248,8 @@ def tile_moe_cpy_mlp_silu_kernel(
 
         for lo, size, where, copy in (
             (0, 2 * C, 1, nc.scalar.copy),
-            (2 * C, C, 2, nc.vector.tensor_copy),
-            (3 * C, C, 3, nc.scalar.copy),
+            (2 * C, C + P, 2, nc.vector.tensor_copy),
+            (S - P, P, 3, nc.scalar.copy),
         ):
             acc = bank(where, [P, size])
             second_layer(acc, 0, lo, size)

@@ -31,6 +31,7 @@ TG = TV + P
 
 SHIFT = 16
 W1_LOADS = [(0, 1), (1, 1), (2, 2)]
+W2_LOADS = [(0, 2), (2, 2), (4, 4)]
 GROUPS = [(0, C), (C, C), (2 * C, C), (3 * C, P), (S - P, P)]
 
 
@@ -50,7 +51,7 @@ def tile_moe_cpy_mlp_silu_kernel(
         offs_t = lists.tile([P, S // 16], U16, name="offs_t")
         pos_t = [lists.tile([P, T // 16], U16, name=f"pos_t{r}") for r in range(2)]
 
-        xw = [keep.tile([P, T], I32, name=f"xw{s}", align_bytes=64) for s in range(2)]
+        xw = [keep.tile([P, T], I32, name=f"xw{s}", tag=f"xw{s}", align_bytes=64) for s in range(2)]
         xs = keep.tile([P, T], U8, name="xs", align_bytes=64)
         scales = keep.tile([P, S], U8, name="scales", align_bytes=64)
         moved = keep.tile([P, S], U8, name="moved", align_bytes=64)
@@ -61,7 +62,7 @@ def tile_moe_cpy_mlp_silu_kernel(
         w1p = {e0 + j: w1p_tiles[e0][:, j * 4 * H : (j + 1) * 4 * H] for e0, n in W1_LOADS[1:] for j in range(n)}
         w1ps = {e: keep.tile([P, 2 * H], U8, name=f"w1ps{e}", align_bytes=64) for e in (1, 2)}
         w1s = keep.tile([P, E * 2 * H], U8, name="w1s", align_bytes=64)
-        w2 = [keep.tile([P, E * K], U8, name=f"w2_{h}", align_bytes=64) for h in range(2)]
+        w2 = {n0: keep.tile([P, E * blocks * 2 * P], U8, name=f"w2_{n0}", align_bytes=64) for n0, blocks in W2_LOADS}
         w2s = keep.tile([P, E * K], U8, name="w2s", align_bytes=64)
         y = [keep.tile([P, W], F32, name=f"y{n}") for n in range(NB)]
         ident = keep.tile([P, P], F32, name="ident")
@@ -90,10 +91,10 @@ def tile_moe_cpy_mlp_silu_kernel(
                 w1_words[e0 : e0 + n].bitcast(I32).rearrange("e s p i -> p (e s) i"),
             )
 
-        def load_w2(h):
+        def load_w2(n0, blocks):
             nc.sync.dma_start(
-                w2[h][:].bitcast(I32).rearrange("p (e n) -> p e n", e=E),
-                w2_words.bitcast(I32).rearrange("e s p n -> p (e s) n")[:, :, h * (K // 4) : (h + 1) * (K // 4)],
+                w2[n0][:].bitcast(I32).rearrange("p (e n) -> p e n", e=E),
+                w2_words.bitcast(I32).rearrange("e s p n -> p (e s) n")[:, :, n0 * P // 2 : (n0 + blocks) * P // 2],
             )
 
         def load_xr(n):
@@ -116,16 +117,19 @@ def tile_moe_cpy_mlp_silu_kernel(
         nc.sync.dma_start(pos_t[0][:], pos1)
         nc.sync.dma_start(pos_t[1][:], pos2)
         load_scale_rows(w2s, w2_scales.bitcast(I32).rearrange("e s b n -> b (e s) n"), (nc.sync,))
-        load_w2(0)
+        load_w2(*W2_LOADS[0])
         load_xr(0)
-        nc.sync.dma_start(g[:], gate.rearrange("r p t -> p r t")[:, :, 0:TG])
+        gate_rows = gate.rearrange("r p t -> p r t")
+        nc.sync.dma_start(g[:, :, 0:TV], gate_rows[:, :, 0:TV])
         load_xr(1)
-        load_w2(1)
+        load_w2(*W2_LOADS[1])
+        load_w2(*W2_LOADS[2])
         with nc.allow_non_contiguous_dma(reason="one gate value a token and partition"):
             for r in range(2):
                 nc.sync.dma_start(gT[r][:], gate[r, 0, TV:T].rearrange("(c p) -> p c", p=P))
         for n in range(2, NB):
             load_xr(n)
+        nc.sync.dma_start(g[:, :, TV:TG], gate_rows[:, :, TV:TG])
 
         def order_scales(e):
             nc.gpsimd.tensor_copy(
@@ -141,27 +145,33 @@ def tile_moe_cpy_mlp_silu_kernel(
 
         slot_words = {}
 
-        def gather_words(words, first, slots, runs):
-            for at, size, s in runs:
-                lo = first + at
+        def gather_words(words, s, first, sizes):
+            lo = first
+            for size in sizes:
                 nc.vector.tensor_copy(
-                    words[:, s * slots + at : s * slots + at + size],
+                    words[:, lo - first : lo - first + size],
                     xw[s][:].bitcast(U32).indirect(offs_t[:, lo // 16 : (lo + size) // 16]),
                 )
-            for at in range(0, slots, P):
-                for s in range(2):
-                    slot_words[first + at, s] = words[:, s * slots + at : s * slots + at + P]
+                for at in range(lo, lo + size, P):
+                    slot_words[at, s] = words[:, at - first : at - first + P]
+                lo = lo + size
 
         order_scales(1)
         order_scales(2)
-        order_words(1, nc.scalar.copy)
-        early = keep.tile([P, 4 * C], U32, name="early", align_bytes=64)
-        gather_words(early, 0, 2 * C, [(at, size, s) for s in range(2) for at, size in ((0, P), (P, P), (C, C))])
+        for s in range(2):
+            nc.scalar.copy(
+                w1p[1][:, s * 2 * H : (s + 1) * 2 * H].bitcast(U16).rearrange("p (t m) -> p t m", t=4),
+                w1[1][:, s * 2 * H : (s + 1) * 2 * H].bitcast(U16).rearrange("p (m t) -> p t m", t=4),
+            )
+        gather_words(keep.tile([P, 3 * C], U32, name="pass0", align_bytes=64), 0, 0, (P, P, C, C))
+        gather_words(keep.tile([P, 2 * C], U32, name="early", align_bytes=64), 1, 0, (P, P, C))
         order_words(2, nc.vector.tensor_copy)
         w1ps[3] = reuse.tile([P, 2 * H], U8, name="w1ps3", offset=0, align_bytes=64)
         order_scales(3)
-        late = reuse.tile([P, 4 * C], U32, name="late", offset=2 * H, align_bytes=64)
-        gather_words(late, 2 * C, 2 * C, [(at, P, s) for at in range(0, 2 * C, P) for s in range(2)])
+        late = reuse.tile([P, 3 * C], U32, name="late", offset=2 * H, align_bytes=64)
+        gather_words(late[:, 0:C], 1, 2 * C, (P, P))
+        gather_words(late[:, C : 2 * C], 0, 3 * C, (C,))
+        gather_words(late[:, 2 * C : 3 * C], 1, 3 * C, (P, P))
 
         hq = keep.tile([P, 4 * S], BF16, name="hq", align_bytes=64)
         codes = keep.tile([P, S], U32, name="codes", align_bytes=64)
@@ -230,14 +240,14 @@ def tile_moe_cpy_mlp_silu_kernel(
             quantise(*GROUPS[i])
 
         def second_layer(acc, n, lo, size):
-            h, m = divmod(n, NB // 2)
+            n0, blocks = [load for load in W2_LOADS if load[0] <= n][-1]
             done = 0
             while done < size:
                 e, at = divmod(lo + done, C)
                 run = min(C - at, size - done)
                 nc.tensor.matmul_mx(
                     out=acc[:, done : done + run],
-                    lhsT=w2[h][:, e * K + m * 2 * P : e * K + (m + 1) * 2 * P].bitcast(FP4X4),
+                    lhsT=w2[n0][:, (e * blocks + n - n0) * 2 * P : (e * blocks + n - n0 + 1) * 2 * P].bitcast(FP4X4),
                     lhsT_scale=w2s[:, e * K + n * P : e * K + (n + 1) * P],
                     rhs=codes[:, lo + done : lo + done + run].bitcast(FP8X4),
                     rhs_scale=cs[:, lo + done : lo + done + run],

@@ -32,6 +32,7 @@ TG = TV + P
 SHIFT = 16
 W1_LOADS = [(0, 1), (1, 1), (2, 2)]
 W2_LOADS = [(0, 2), (2, 2), (4, 4)]
+W2_SETS = [(0, 2), (2, 6)]
 GROUPS = [(0, C), (C, C), (2 * C, C), (3 * C, P), (S - P, P)]
 
 
@@ -60,10 +61,10 @@ def tile_moe_cpy_mlp_silu_kernel(
         w1 = {e0 + j: w1_tiles[e0][:, j * 4 * H : (j + 1) * 4 * H] for e0, n in W1_LOADS for j in range(n)}
         w1p_tiles = {e0: keep.tile([P, n * 4 * H], U8, name=f"w1p{e0}", align_bytes=64) for e0, n in W1_LOADS[1:]}
         w1p = {e0 + j: w1p_tiles[e0][:, j * 4 * H : (j + 1) * 4 * H] for e0, n in W1_LOADS[1:] for j in range(n)}
-        w1ps = {e: keep.tile([P, 2 * H], U8, name=f"w1ps{e}", align_bytes=64) for e in (1, 2)}
+        w1ps = {e: keep.tile([P, 2 * H], U8, name=f"w1ps{e}", align_bytes=64) for e in range(1, E)}
         w1s = keep.tile([P, E * 2 * H], U8, name="w1s", align_bytes=64)
         w2 = {n0: keep.tile([P, E * blocks * 2 * P], U8, name=f"w2_{n0}", align_bytes=64) for n0, blocks in W2_LOADS}
-        w2s = keep.tile([P, E * K], U8, name="w2s", align_bytes=64)
+        w2s = {n0: keep.tile([P, E * blocks * P], U8, name=f"w2s{n0}", align_bytes=64) for n0, blocks in W2_SETS}
         y = [keep.tile([P, W], F32, name=f"y{n}") for n in range(NB)]
         ident = keep.tile([P, P], F32, name="ident")
         g = keep.tile([P, 2, TG], F32, name="g")
@@ -74,7 +75,8 @@ def tile_moe_cpy_mlp_silu_kernel(
         nc.vector.memset(moved[96:P, :].bitcast(I32), 0)
         nc.vector.memset(y[0][:, S + T : W], 0.0)
         make_identity(nc, ident[:])
-        nc.gpsimd.memset(w2s[:].bitcast(I32), 0)
+        for tile in w2s.values():
+            nc.gpsimd.memset(tile[:].bitcast(I32), 0)
         nc.scalar.activation(y[1][:, S + T : W], y[0][:, S + T : W], SILU)
         for n in range(2, NB):
             nc.scalar.copy(y[n][:, S + T : W], y[0][:, S + T : W])
@@ -116,12 +118,14 @@ def tile_moe_cpy_mlp_silu_kernel(
             queue.dma_start(moved[0 : P - SHIFT, lo:hi].bitcast(I32), scales[SHIFT:P, lo:hi].bitcast(I32))
         nc.sync.dma_start(pos_t[0][:], pos1)
         nc.sync.dma_start(pos_t[1][:], pos2)
-        load_scale_rows(w2s, w2_scales.bitcast(I32).rearrange("e s b n -> b (e s) n"), (nc.sync,))
+        w2_rows = w2_scales.bitcast(I32).rearrange("e s b n -> b (e s) n")
+        load_scale_rows(w2s[0], w2_rows[:, :, 0 : 2 * P // 4], (nc.sync,))
         load_w2(*W2_LOADS[0])
         load_xr(0)
         gate_rows = gate.rearrange("r p t -> p r t")
         nc.sync.dma_start(g[:, :, 0:TV], gate_rows[:, :, 0:TV])
         load_xr(1)
+        load_scale_rows(w2s[2], w2_rows[:, :, 2 * P // 4 : K // 4], (nc.sync,))
         load_w2(*W2_LOADS[1])
         load_w2(*W2_LOADS[2])
         with nc.allow_non_contiguous_dma(reason="one gate value a token and partition"):
@@ -135,12 +139,6 @@ def tile_moe_cpy_mlp_silu_kernel(
             nc.gpsimd.tensor_copy(
                 w1ps[e][:].rearrange("p (s t m) -> p s t m", s=2, t=4),
                 w1s[:, 2 * e * H : 2 * (e + 1) * H].rearrange("p (s m t) -> p s t m", s=2, t=4),
-            )
-
-        def order_words(e0, copy):
-            copy(
-                w1p_tiles[e0][:].bitcast(U16).rearrange("p (a t m) -> p a t m", t=4, m=P),
-                w1_tiles[e0][:].bitcast(U16).rearrange("p (a m t) -> p a t m", t=4, m=P),
             )
 
         slot_words = {}
@@ -158,20 +156,22 @@ def tile_moe_cpy_mlp_silu_kernel(
 
         order_scales(1)
         order_scales(2)
+        order_scales(3)
         for s in range(2):
             nc.scalar.copy(
                 w1p[1][:, s * 2 * H : (s + 1) * 2 * H].bitcast(U16).rearrange("p (t m) -> p t m", t=4),
                 w1[1][:, s * 2 * H : (s + 1) * 2 * H].bitcast(U16).rearrange("p (m t) -> p t m", t=4),
             )
         gather_words(keep.tile([P, 3 * C], U32, name="pass0", align_bytes=64), 0, 0, (P, P, C, C))
-        gather_words(keep.tile([P, 2 * C], U32, name="early", align_bytes=64), 1, 0, (P, P, C))
-        order_words(2, nc.vector.tensor_copy)
-        w1ps[3] = reuse.tile([P, 2 * H], U8, name="w1ps3", offset=0, align_bytes=64)
-        order_scales(3)
-        late = reuse.tile([P, 3 * C], U32, name="late", offset=2 * H, align_bytes=64)
-        gather_words(late[:, 0:C], 1, 2 * C, (P, P))
-        gather_words(late[:, C : 2 * C], 0, 3 * C, (C,))
-        gather_words(late[:, 2 * C : 3 * C], 1, 3 * C, (P, P))
+        gather_words(keep.tile([P, 3 * C], U32, name="early", align_bytes=64), 1, 0, (P, P, C, C))
+        for e in (2, 3):
+            nc.vector.tensor_copy(
+                w1p[e].bitcast(U16).rearrange("p (s t m) -> p s t m", s=2, t=4),
+                w1[e].bitcast(U16).rearrange("p (s m t) -> p s t m", s=2, t=4),
+            )
+        late = reuse.tile([P, 2 * C], U32, name="late", offset=0, align_bytes=64)
+        gather_words(late[:, 0:C], 0, 3 * C, (C,))
+        gather_words(late[:, C : 2 * C], 1, 3 * C, (P, P))
 
         hq = keep.tile([P, 4 * S], BF16, name="hq", align_bytes=64)
         codes = keep.tile([P, S], U32, name="codes", align_bytes=64)
@@ -241,6 +241,7 @@ def tile_moe_cpy_mlp_silu_kernel(
 
         def second_layer(acc, n, lo, size):
             n0, blocks = [load for load in W2_LOADS if load[0] <= n][-1]
+            s0, width = [part for part in W2_SETS if part[0] <= n][-1]
             done = 0
             while done < size:
                 e, at = divmod(lo + done, C)
@@ -248,7 +249,7 @@ def tile_moe_cpy_mlp_silu_kernel(
                 nc.tensor.matmul_mx(
                     out=acc[:, done : done + run],
                     lhsT=w2[n0][:, (e * blocks + n - n0) * 2 * P : (e * blocks + n - n0 + 1) * 2 * P].bitcast(FP4X4),
-                    lhsT_scale=w2s[:, e * K + n * P : e * K + (n + 1) * P],
+                    lhsT_scale=w2s[s0][:, (e * width + n - s0) * P : (e * width + n - s0 + 1) * P],
                     rhs=codes[:, lo + done : lo + done + run].bitcast(FP8X4),
                     rhs_scale=cs[:, lo + done : lo + done + run],
                     start=True,

from contextlib import ExitStack

import concourse.mybir as mybir
from concourse.masks import make_identity

K, T, E, C, H, PAD = 1024, 768, 4, 256, 512, 64
S = E * C
W = S + T + PAD
P = 128
NB = K // P
FLOPS = 2 * 2 * S * K * H

F32 = mybir.dt.float32
BF16 = mybir.dt.bfloat16
I32 = mybir.dt.int32
U32 = mybir.dt.uint32
U16 = mybir.dt.uint16
U8 = mybir.dt.uint8
FP8X4 = mybir.dt.float8_e4m3fn_x4
FP4X4 = mybir.dt.float4_e2m1fn_x4
MULT = mybir.AluOpType.mult
ADD = mybir.AluOpType.add
SILU = mybir.ActivationFunctionType.Silu
COPY = mybir.ActivationFunctionType.Copy

TV = 512
TS = T - TV
CH = TS // P
PAIRS = [((0, 1), 0), ((2, 3), 0), ((4, 5), 0), ((6,), 0), ((7,), 1)]
TG = TV + P

SHIFT = 16
W1_LOADS = [(0, 1), (1, 1), (2, 2)]
W2_LOADS = [(0, 2), (2, 2), (4, 4)]
W2_SETS = [(0, 2), (2, 6)]
GROUPS = [(0, C), (C, C), (2 * C, C), (3 * C, P), (S - P, P)]


def tile_moe_cpy_mlp_silu_kernel(
    tc, x_words, x_scales, xr, w1_words, w1_scales, w2_words, w2_scales, gate, offs, pos1, pos2, out
):
    nc = tc.nc
    with ExitStack() as ctx:
        lists = ctx.enter_context(tc.tile_pool(name="lists", bufs=1))
        keep = ctx.enter_context(tc.tile_pool(name="keep", bufs=1))
        reuse = ctx.enter_context(tc.tile_pool(name="reuse", bufs=1))
        psum = ctx.enter_context(tc.psum_pool(name="psum", bufs=1))

        def bank(i, shape):
            return psum.tile(shape, F32, name=f"bank{i}", tag=f"bank{i}")

        offs_t = lists.tile([P, S // 16], U16, name="offs_t")
        pos_t = [lists.tile([P, T // 16], U16, name=f"pos_t{r}") for r in range(2)]

        xw = [keep.tile([P, T], I32, name=f"xw{s}", tag=f"xw{s}", align_bytes=64) for s in range(2)]
        xs = keep.tile([P, T], U8, name="xs", align_bytes=64)
        scales = keep.tile([P, S], U8, name="scales", align_bytes=64)
        moved = keep.tile([P, S], U8, name="moved", align_bytes=64)
        w1_tiles = {e: keep.tile([P, 4 * H], U8, name=f"w1_{e}", align_bytes=64) for e in range(2)}
        w1_tiles[2] = reuse.tile([P, 8 * H], U8, name="w1_2", offset=0, align_bytes=64)
        w1 = {e0 + j: w1_tiles[e0][:, j * 4 * H : (j + 1) * 4 * H] for e0, n in W1_LOADS for j in range(n)}
        w1p_tiles = {e0: keep.tile([P, n * 4 * H], U8, name=f"w1p{e0}", align_bytes=64) for e0, n in W1_LOADS[1:]}
        w1p = {e0 + j: w1p_tiles[e0][:, j * 4 * H : (j + 1) * 4 * H] for e0, n in W1_LOADS[1:] for j in range(n)}
        w1ps = {e: keep.tile([P, 2 * H], U8, name=f"w1ps{e}", align_bytes=64) for e in range(1, E)}
        w1s = keep.tile([P, E * 2 * H], U8, name="w1s", align_bytes=64)
        w2 = {n0: keep.tile([P, E * blocks * 2 * P], U8, name=f"w2_{n0}", align_bytes=64) for n0, blocks in W2_LOADS}
        w2s = {n0: keep.tile([P, E * blocks * P], U8, name=f"w2s{n0}", align_bytes=64) for n0, blocks in W2_SETS}
        y = [keep.tile([P, W], F32, name=f"y{n}") for n in range(NB)]
        ident = keep.tile([P, P], F32, name="ident")
        g = keep.tile([P, 2, TG], F32, name="g")
        gT = [keep.tile([P, CH], F32, name=f"gT{r}") for r in range(2)]

        nc.gpsimd.memset(xs[:].bitcast(I32), 0)
        nc.vector.memset(w1s[:].bitcast(I32), 0)
        nc.vector.memset(moved[96:P, :].bitcast(I32), 0)
        nc.vector.memset(y[0][:, S + T : W], 0.0)
        make_identity(nc, ident[:])
        for tile in w2s.values():
            nc.gpsimd.memset(tile[:].bitcast(I32), 0)
        nc.scalar.activation(y[1][:, S + T : W], y[0][:, S + T : W], SILU)
        for n in range(2, NB):
            nc.scalar.copy(y[n][:, S + T : W], y[0][:, S + T : W])

        def load_scale_rows(tile, rows, queues):
            for r in range(4):
                queues[r % len(queues)].dma_start(
                    tile[r:P:32, :].bitcast(I32).rearrange("q (a i) -> q a i", a=rows.shape[1]), rows[r:16:4]
                )

        def load_w1(e0, n):
            nc.sync.dma_start(
                w1_tiles[e0][:].bitcast(I32).rearrange("p (a i) -> p a i", a=2 * n),
                w1_words[e0 : e0 + n].bitcast(I32).rearrange("e s p i -> p (e s) i"),
            )

        def load_w2(n0, blocks):
            nc.sync.dma_start(
                w2[n0][:].bitcast(I32).rearrange("p (e n) -> p e n", e=E),
                w2_words.bitcast(I32).rearrange("e s p n -> p (e s) n")[:, :, n0 * P // 2 : (n0 + blocks) * P // 2],
            )

        def load_xr(n):
            nc.sync.dma_start(y[n][:, S : S + T], xr[n * P : (n + 1) * P, :])

        nc.sync.dma_start(offs_t[:], offs)
        xs_rows = x_scales.bitcast(I32).rearrange("s b t -> b s t")
        for r in range(4):
            (nc.sync, nc.scalar)[r % 2].dma_start(xs[r:P:SHIFT, :].bitcast(I32), xs_rows[r:16:4])
        token_words = x_words.rearrange("s p t d -> s p (t d)").bitcast(I32)
        nc.sync.dma_start(xw[0][:], token_words[0])
        load_scale_rows(w1s, w1_scales.bitcast(I32).rearrange("e s b i -> b (e s) i"), (nc.sync,))
        load_w1(*W1_LOADS[0])
        load_w1(*W1_LOADS[1])
        nc.sync.dma_start(xw[1][:], token_words[1])
        load_w1(*W1_LOADS[2])
        for lo, hi, queue in ((0, C, nc.scalar), (C, 2 * C, nc.scalar), (2 * C, S, nc.sync)):
            nc.vector.tensor_copy(scales[:, lo:hi], xs[:].indirect(offs_t[:, lo // 16 : hi // 16]))
            queue.dma_start(moved[0 : P - SHIFT, lo:hi].bitcast(I32), scales[SHIFT:P, lo:hi].bitcast(I32))
        nc.sync.dma_start(pos_t[0][:], pos1)
        nc.sync.dma_start(pos_t[1][:], pos2)
        w2_rows = w2_scales.bitcast(I32).rearrange("e s b n -> b (e s) n")
        load_scale_rows(w2s[0], w2_rows[:, :, 0 : 2 * P // 4], (nc.sync,))
        load_w2(*W2_LOADS[0])
        load_xr(0)
        gate_rows = gate.rearrange("r p t -> p r t")
        nc.sync.dma_start(g[:, :, 0:TV], gate_rows[:, :, 0:TV])
        load_xr(1)
        load_scale_rows(w2s[2], w2_rows[:, :, 2 * P // 4 : K // 4], (nc.sync,))
        load_w2(*W2_LOADS[1])
        load_w2(*W2_LOADS[2])
        with nc.allow_non_contiguous_dma(reason="one gate value a token and partition"):
            for r in range(2):
                nc.sync.dma_start(gT[r][:], gate[r, 0, TV:T].rearrange("(c p) -> p c", p=P))
        for n in range(2, NB):
            load_xr(n)
        nc.sync.dma_start(g[:, :, TV:TG], gate_rows[:, :, TV:TG])

        def order_scales(e):
            nc.gpsimd.tensor_copy(
                w1ps[e][:].rearrange("p (s t m) -> p s t m", s=2, t=4),
                w1s[:, 2 * e * H : 2 * (e + 1) * H].rearrange("p (s m t) -> p s t m", s=2, t=4),
            )

        slot_words = {}

        def gather_words(words, s, first, sizes):
            lo = first
            for size in sizes:
                nc.vector.tensor_copy(
                    words[:, lo - first : lo - first + size],
                    xw[s][:].bitcast(U32).indirect(offs_t[:, lo // 16 : (lo + size) // 16]),
                )
                for at in range(lo, lo + size, P):
                    slot_words[at, s] = words[:, at - first : at - first + P]
                lo = lo + size

        order_scales(1)
        order_scales(2)
        order_scales(3)
        for s in range(2):
            nc.scalar.copy(
                w1p[1][:, s * 2 * H : (s + 1) * 2 * H].bitcast(U16).rearrange("p (t m) -> p t m", t=4),
                w1[1][:, s * 2 * H : (s + 1) * 2 * H].bitcast(U16).rearrange("p (m t) -> p t m", t=4),
            )
        gather_words(keep.tile([P, 3 * C], U32, name="pass0", align_bytes=64), 0, 0, (P, P, C, C))
        gather_words(keep.tile([P, 3 * C], U32, name="early", align_bytes=64), 1, 0, (P, P, C, C))
        for e in (2, 3):
            nc.vector.tensor_copy(
                w1p[e].bitcast(U16).rearrange("p (s t m) -> p s t m", s=2, t=4),
                w1[e].bitcast(U16).rearrange("p (s m t) -> p s t m", s=2, t=4),
            )
        late = reuse.tile([P, 2 * C], U32, name="late", offset=0, align_bytes=64)
        gather_words(late[:, 0:C], 0, 3 * C, (C,))
        gather_words(late[:, C : 2 * C], 1, 3 * C, (P, P))

        hq = keep.tile([P, 4 * S], BF16, name="hq", align_bytes=64)
        codes = keep.tile([P, S], U32, name="codes", align_bytes=64)
        cs = keep.tile([P, S], U8, name="cs", align_bytes=64)

        def quantise(lo, size):
            nc.vector.quantize_mx(
                out=codes[:, lo : lo + size].bitcast(FP8X4),
                scales=cs[:, lo : lo + size],
                in_=hq[:, 4 * lo : 4 * (lo + size)],
            )

        def first_layer(lo):
            e = lo // C
            pre = bank(lo // P, [P, 4, P])
            for s in range(2):
                for t in range(4):
                    at = s * H + t * P
                    nc.tensor.matmul_mx(
                        out=pre[:, t, :],
                        lhsT=w1p[e][:, 2 * at : 2 * (at + P)].bitcast(FP4X4),
                        lhsT_scale=w1ps[e][:, at : at + P],
                        rhs=slot_words[lo, s].bitcast(FP8X4),
                        rhs_scale=(scales, moved)[s][:, lo : lo + P],
                        start=(s == 0 and t == 0),
                        stop=(s == 1 and t == 3),
                    )
            nc.scalar.activation(
                hq[:, 4 * lo : 4 * (lo + P)].rearrange("p (s t) -> p s t", t=4),
                pre[:].rearrange("p t s -> p s t"),
                SILU,
            )

        hb = keep.tile([P, 2, H], BF16, name="hb")
        for b in range(2):
            pre = bank(b, [P, H])
            for s in range(2):
                nc.tensor.matmul_mx(
                    out=pre[:],
                    lhsT=slot_words[b * P, s].bitcast(FP8X4),
                    lhsT_scale=(scales, moved)[s][:, b * P : (b + 1) * P],
                    rhs=w1[0][:, s * 2 * H : (s + 1) * 2 * H].bitcast(FP4X4),
                    rhs_scale=w1s[:, s * H : (s + 1) * H],
                    start=(s == 0),
                    stop=(s == 1),
                )
            nc.scalar.activation(
                hb[:, b, :].rearrange("s (u p d) -> s u p d", u=2, d=2),
                pre[:].rearrange("s (p u d) -> s u p d", u=2, d=2),
                SILU,
            )
        for lo in range(C, 2 * C, P):
            first_layer(lo)
        hT = bank(0, [P, 2, 2, P])
        for b in range(2):
            pairs = hb[:, b, :].bitcast(F32)
            for u in range(2):
                nc.tensor.transpose(hT[:, b, u, :], pairs[:, u * P : (u + 1) * P], ident[:])
        nc.scalar.copy(
            hq[:, 0 : 4 * C].bitcast(F32).rearrange("p (b s u) -> p b s u", b=2, u=2),
            hT[:].rearrange("p b u s -> p b s u"),
        )
        for lo in range(2 * C, S, P):
            first_layer(lo)
        for i in (1, 0, 2, 3, 4):
            quantise(*GROUPS[i])

        def second_layer(acc, n, lo, size):
            n0, blocks = [load for load in W2_LOADS if load[0] <= n][-1]
            s0, width = [part for part in W2_SETS if part[0] <= n][-1]
            done = 0
            while done < size:
                e, at = divmod(lo + done, C)
                run = min(C - at, size - done)
                nc.tensor.matmul_mx(
                    out=acc[:, done : done + run],
                    lhsT=w2[n0][:, (e * blocks + n - n0) * 2 * P : (e * blocks + n - n0 + 1) * 2 * P].bitcast(FP4X4),
                    lhsT_scale=w2s[s0][:, (e * width + n - s0) * P : (e * width + n - s0 + 1) * P],
                    rhs=codes[:, lo + done : lo + done + run].bitcast(FP8X4),
                    rhs_scale=cs[:, lo + done : lo + done + run],
                    start=True,
                    stop=True,
                )
                done = done + run

        for lo, size, where, copy in (
            (0, 2 * C, 1, nc.scalar.copy),
            (2 * C, C + P, 2, nc.vector.tensor_copy),
            (S - P, P, 3, nc.scalar.copy),
        ):
            acc = bank(where, [P, size])
            second_layer(acc, 0, lo, size)
            copy(y[0][:, lo : lo + size], acc[:])

        def slots_of(n, first_bank):
            for lo in range(0, S, 2 * C):
                acc = bank(first_bank + lo // (2 * C), [P, 2 * C])
                second_layer(acc, n, lo, 2 * C)
                nc.scalar.copy(y[n][:, lo : lo + 2 * C], acc[:])

        for n, first_bank in zip(range(1, NB), (4, 6, 0, 2, 4, 6, 0)):
            slots_of(n, first_bank)

        def weighted(n, r, lo, size):
            a = keep.tile([P, size], F32, name=f"a{n}_{r}_{lo}")
            nc.vector.tensor_tensor(
                a[:], y[n][:].indirect(pos_t[r][:, lo // 16 : (lo + size) // 16]), g[:, r, lo : lo + size], MULT
            )
            return a

        def add_and_store(n, first, second, lo, size):
            res = keep.tile([P, size], F32, name=f"res{n}_{lo}")
            nc.vector.tensor_tensor(res[:], first, second, ADD)
            nc.sync.dma_start(out[n * P : (n + 1) * P, lo : lo + size], res[:])

        mine = {n: TV + c0 * P for blocks, c0 in PAIRS for n in blocks}
        first = weighted(0, 0, 0, mine[0])
        for n in range(NB - 1):
            second = weighted(n, 1, 0, mine[n])
            coming = weighted(n + 1, 0, 0, mine[n + 1])
            add_and_store(n, first[:], second[:], 0, mine[n])
            first = coming
        half = mine[NB - 1] // 2
        halves = [weighted(NB - 1, 1, lo, half) for lo in (0, half)]
        for i, lo in enumerate((0, half)):
            add_and_store(NB - 1, first[:, lo : lo + half], halves[i][:], lo, half)

        def fetch(k):
            blocks, c0 = PAIRS[k]
            lo = TV + c0 * P
            got = keep.tile([P, 2, len(blocks), T - lo], F32, name=f"got{k}")
            turned = []
            for r in range(2):
                for b, n in enumerate(blocks):
                    nc.scalar.activation(got[:, r, b, :], y[n][:].indirect(pos_t[r][:, lo // 16 : T // 16]), COPY)
                tT = bank((2, 6, 0)[k % 3] + r, [P, CH - c0, len(blocks), P])
                for c in range(CH - c0):
                    for b in range(len(blocks)):
                        nc.tensor.transpose(tT[:, c, b, :], got[:, r, b, c * P : (c + 1) * P], ident[:])
                turned.append(tT)
            return turned

        def weigh(k, turned):
            blocks, c0 = PAIRS[k]
            chunks = CH - c0
            u = keep.tile([P, 2, chunks, len(blocks), P], F32, name=f"u{k}")
            back = bank(4 + k % 2, [P, len(blocks), chunks * P])
            for r in range(2):
                for c in range(chunks):
                    nc.scalar.activation(
                        u[:, r, c].rearrange("p b n -> p (b n)"),
                        turned[r][:, c].rearrange("p b n -> p (b n)"),
                        COPY,
                        scale=gT[r][:, c0 + c : c0 + c + 1],
                    )
                    for b in range(len(blocks)):
                        nc.tensor.matmul(
                            back[:, b, c * P : (c + 1) * P], u[:, r, c, b, :], ident[:],
                            start=(r == 0 and c == 0 and b == 0),
                            stop=(r == 1 and c == chunks - 1 and b == len(blocks) - 1),
                            is_transpose=True,
                        )
            return back

        def leave(k, back):
            blocks, c0 = PAIRS[k]
            lo = TV + c0 * P
            res = keep.tile([P, len(blocks), T - lo], F32, name=f"left{k}")
            nc.scalar.copy(res[:], back[:])
            rows = out[blocks[0] * P : (blocks[-1] + 1) * P, lo:T]
            nc.scalar.dma_start(rows.rearrange("(b p) t -> p b t", p=P), res[:])

        turned = {0: fetch(0)}
        backs = {}
        for k in range(len(PAIRS)):
            if k + 1 < len(PAIRS):
                turned[k + 1] = fetch(k + 1)
            if k > 0:
                leave(k - 1, backs[k - 1])
            backs[k] = weigh(k, turned[k])
        leave(len(PAIRS) - 1, backs[len(PAIRS) - 1])
